import numpy as np
import ml_dtypes


def mxq(x, axis, fmt="e4m3"):
    dtype, down = {"e4m3": (ml_dtypes.float8_e4m3fn, 7), "e5m2": (ml_dtypes.float8_e5m2, 14)}[fmt]
    v = np.moveaxis(np.asarray(x, np.float32).astype(ml_dtypes.bfloat16).astype(np.float64), axis, -1)
    blocks = v.reshape(v.shape[:-1] + (-1, 32))
    amax = np.abs(blocks).max(-1, keepdims=True)
    byte = np.maximum(np.where(amax > 0, np.frexp(amax)[1] - 1 + 127, 0) - down, 1)
    scale = np.exp2(byte - 127.0)
    codes = (blocks / scale).astype(np.float32).astype(dtype).astype(np.float64)
    return np.moveaxis((codes * scale).reshape(v.shape), -1, axis)


WIDE = False


def mx_kscale(k):
    if not WIDE:
        return np.ones(k)
    levels = np.array([10, -10, 5, -5, 0])
    if k % 512:
        return np.exp2(np.random.permutation(np.resize(levels, k // 32))).repeat(32)
    a = np.empty((k // 512, 16))
    for p in range(k // 512):
        a[p, :8] = np.random.permutation(np.resize(levels, 8))
        for g in range(8):
            far = levels[np.abs(levels - a[p, g]) >= 10]
            a[p, g + 8] = far[np.random.randint(len(far))]
    return np.exp2(a.ravel()).repeat(32)


def f64(x):
    return np.asarray(x).astype(np.float64)


def striped(idx):
    return np.tile(idx.reshape(-1, 16).T, (8, 1)).astype(np.uint16)


def unstriped(offs):
    return offs[:16].T.reshape(-1).astype(np.int64)


E2M1 = np.array([0.0, 0.5, 1.0, 1.5, 2.0, 3.0, 4.0, 6.0, -0.0, -0.5, -1.0, -1.5, -2.0, -3.0, -4.0, -6.0])


def pack_weight(w, fmt):
    k, n = w.shape
    w = f64(np.asarray(w, np.float32).astype(ml_dtypes.bfloat16)).reshape(k // 32, 32, n)
    amax = np.abs(w).max(1)
    if fmt == "e4m3":
        byte = np.frexp(amax)[1] - 1 + 127 - 7
    else:
        mant, ex = np.frexp(amax / 6.0)
        byte = np.where(mant > 0.5, ex, ex - 1) + 127
    byte = np.clip(np.where(amax > 0, byte, 1), 1, 254)
    scaled = (w * np.exp2(127.0 - byte)[:, None, :]).reshape(k, n).astype(np.float32)
    by_word = np.ascontiguousarray(scaled.reshape(k // 512, 128, 4, n).transpose(0, 1, 3, 2))
    if fmt == "e4m3":
        words = by_word.astype(ml_dtypes.float8_e4m3fn).view(np.uint8)
    else:
        c = by_word.astype(ml_dtypes.float4_e2m1fn).view(np.uint8) & 0xF
        words = (c[..., 0::2] | (c[..., 1::2] << 4)).reshape(k // 512, 128, 2 * n)
    return np.ascontiguousarray(words), np.ascontiguousarray(byte.astype(np.uint8).reshape(k // 512, 16, n))


def unpack_weight(words, scales, fmt):
    g, _, n = scales.shape
    words = np.ascontiguousarray(words).reshape(g, 128, n, -1)
    if fmt == "e4m3":
        vals = words.view(ml_dtypes.float8_e4m3fn).astype(np.float64)
    else:
        nib = np.empty((g, 128, n, 4), np.uint8)
        nib[..., 0::2] = words & 0xF
        nib[..., 1::2] = words >> 4
        vals = E2M1[nib]
    vals = vals * np.repeat(np.exp2(scales.astype(np.float64) - 127.0), 8, axis=1)[..., None]
    return vals.transpose(0, 1, 3, 2).reshape(g * 512, n)


def gelu(v):
    return 0.5 * v * (1.0 + np.tanh(np.sqrt(2.0 / np.pi) * (v + 0.044715 * v**3)))


K, K2, K3, H, N, T, T2, T3, S = 1024, 1536, 512, 1024, 512, 2048, 2048, 1024, 512

def setup_inputs():
    n = np.random.standard_normal
    s = mx_kscale(K)[:, None]
    s2 = mx_kscale(K2)[:, None]
    s3 = mx_kscale(K3)[:, None]
    u = mx_kscale(H)[:, None]
    tab_words, tab_scales = pack_weight(n((K, T)) * s, "e4m3")
    tab2_words, tab2_scales = pack_weight(n((K2, T2)) * s2, "e4m3")
    tab3_words, tab3_scales = pack_weight(n((K3, T3)) * s3, "e2m1")
    w1_words, w1_scales = pack_weight(n((K, H)) / np.sqrt(K) / s * u.T, "e2m1")
    w3_words, w3_scales = pack_weight(n((K3, N)) / np.sqrt(K3) / s3, "e4m3")
    w5_words, w5_scales = pack_weight(n((H, N)) / np.sqrt(H) / u, "e2m1")
    return {
        "tab_words": tab_words, "tab_scales": tab_scales,
        "tab2_words": tab2_words, "tab2_scales": tab2_scales,
        "tab3_words": tab3_words, "tab3_scales": tab3_scales,
        "offs": striped(np.random.permutation(T)[:S]),
        "offs2": striped(np.random.permutation(T2)[:S]),
        "offs3": striped(np.random.permutation(T3)[:S]),
        "w1_words": w1_words, "w1_scales": w1_scales,
        "w2": (n((K2, H)) / np.sqrt(K2) / s2 * u.T).astype(np.float32),
        "w3_words": w3_words, "w3_scales": w3_scales,
        "w4": (n((H, N)) / np.sqrt(H) / u).astype(np.float32),
        "w5_words": w5_words, "w5_scales": w5_scales,
    }

def reference(tab_words, tab_scales, tab2_words, tab2_scales, tab3_words, tab3_scales, offs, offs2, offs3, w1_words, w1_scales, w2, w3_words, w3_scales, w4, w5_words, w5_scales):
    v = unpack_weight(tab_words, tab_scales, "e4m3")[:, unstriped(offs)]
    v2 = unpack_weight(tab2_words, tab2_scales, "e4m3")[:, unstriped(offs2)]
    v3 = unpack_weight(tab3_words, tab3_scales, "e2m1")[:, unstriped(offs3)]
    bat = unpack_weight(w1_words, w1_scales, "e2m1").T @ v
    bowl = mxq(f64(w2), 0, "e4m3").T @ v2
    d = bat - bowl
    hp = np.maximum(d, 0.0)
    hn = np.maximum(-d, 0.0)
    yp = mxq(f64(w4), 0, "e4m3").T @ mxq(hp, 0, "e4m3")
    yn = unpack_weight(w5_words, w5_scales, "e2m1").T @ mxq(hn, 0, "e4m3")
    ground = unpack_weight(w3_words, w3_scales, "e4m3").T @ v3
    return yp - yn + ground

@@ -1,0 +1,258 @@
+from contextlib import ExitStack
+
+import concourse.mybir as mybir
+
+F32 = mybir.dt.float32
+BF16 = mybir.dt.bfloat16
+I32 = mybir.dt.int32
+U32 = mybir.dt.uint32
+U16 = mybir.dt.uint16
+U8 = mybir.dt.uint8
+E4M3 = mybir.dt.float8_e4m3fn_x4
+E2M1 = mybir.dt.float4_e2m1fn_x4
+ALU = mybir.AluOpType
+ACT = mybir.ActivationFunctionType
+
+P = 128
+PACK = 4
+K_PASS = P * PACK
+S = 512
+CHUNK = 128
+CHUNKS = S // CHUNK
+N_TILES = 4
+FLOPS = 2 * S * (1024 * 1024 + 1536 * 1024 + 2 * 1024 * 512 + 512 * 512)
+
+
+def tile_list_fixture_surplus_scores_kernel(
+    tc, tab_words, tab_scales, tab2_words, tab2_scales, tab3_words, tab3_scales, offs, offs2, offs3,
+    w1_words, w1_scales, w2, w3_words, w3_scales, w4, w5_words, w5_scales, out,
+):
+    nc = tc.nc
+    with ExitStack() as ctx:
+        keep = ctx.enter_context(tc.tile_pool(name="keep", bufs=1))
+        ring = ctx.enter_context(tc.tile_pool(name="ring", bufs=4))
+        psum = ctx.enter_context(tc.psum_pool(name="psum", bufs=1))
+
+        def held(shape, dtype, name):
+            return keep.tile(shape, dtype, name=name, align_bytes=64)
+
+        def zeroed(shape, name, engine):
+            tile = held(shape, U8, name)
+            engine.memset(tile[:].bitcast(I32), 0)
+            return tile
+
+        tab2_sc = zeroed([P, 2048], "tab2_sc", nc.gpsimd)
+        w1_sc_raw = zeroed([P, 2, 1024], "w1_sc_raw", nc.vector)
+        tab_sc = zeroed([P, 2, 2048], "tab_sc", nc.vector)
+        tab3_sc = zeroed([P, 1, 1024], "tab3_sc", nc.gpsimd)
+        w5_sc = zeroed([P, 2, 512], "w5_sc", nc.gpsimd)
+        w3_sc = zeroed([P, 1, 512], "w3_sc", nc.gpsimd)
+
+        def load_list(src, name):
+            tile = keep.tile([P, S // 16], U16, name=name)
+            nc.sync.dma_start(tile[:], src)
+            return tile
+
+        def load_bytes(src, name):
+            tile = held([P, src.shape[1]], U8, name)
+            nc.sync.dma_start(tile[:].bitcast(I32), src.bitcast(I32))
+            return tile
+
+        def load_scales(tile, src):
+            rows = src.rearrange("a (q r) c -> r q a c", r=4)
+            for r in range(4):
+                nc.sync.dma_start(tile[r:P:32, :, :].bitcast(I32), rows[r].bitcast(I32))
+
+        def load_w2(a, b):
+            tile = held([P, PACK, K_PASS], F32, "w2_raw%d%d" % (a, b))
+            rows = w2[a * K_PASS:(a + 1) * K_PASS, b * K_PASS:(b + 1) * K_PASS]
+            nc.sync.dma_start(tile[:], rows.rearrange("(p i) c -> p i c", i=PACK))
+            return tile
+
+        def load_w4(b):
+            tile = held([P, PACK, K_PASS], F32, "w4_raw%d" % b)
+            nc.sync.dma_start(tile[:], w4[b * K_PASS:(b + 1) * K_PASS, :].rearrange("(p i) c -> p i c", i=PACK))
+            return tile
+
+        def gather(window, offsets, dtype, name):
+            width = {U32: 4, U16: 2, U8: 1}[dtype]
+            tile = held([P, S * width], U8, name)
+            nc.vector.tensor_copy(tile[:].bitcast(dtype), window.bitcast(dtype).indirect(offsets[:]))
+            return tile
+
+        def neg_cast(engine, dst, src, factor):
+            if engine == "scalar":
+                nc.scalar.activation(dst, src, ACT.Copy, scale=factor)
+            else:
+                nc.vector.tensor_scalar(dst, src, factor, None, ALU.mult)
+
+        def quantise(grouped, codes, scales):
+            nc.vector.quantize_mx(out=codes.bitcast(E4M3), scales=scales, in_=grouped)
+
+        def quantise_w2(raw, engines, name):
+            codes = held([P, K_PASS], U32, name + "_codes")
+            scales = held([P, K_PASS], U8, name + "_scales")
+            per = PACK // len(engines)
+            for h, engine in enumerate(engines):
+                grouped = ring.tile([P, per, P, PACK], BF16, name="grouped", align_bytes=64)
+                src = raw[:].rearrange("p i (m t) -> p m i t", t=PACK)[:, :, :, h * per:(h + 1) * per]
+                neg_cast(engine, grouped[:].rearrange("p t m i -> p m i t"), src, -1.0)
+                cols = slice(h * per * P, (h + 1) * per * P)
+                quantise(grouped[:].rearrange("p t m i -> p (t m i)"), codes[:, cols], scales[:, cols])
+            return codes, scales
+
+        def quantise_w4(raw, engines, name):
+            codes = held([P, K_PASS], U32, name + "_codes")
+            scales = held([P, K_PASS], U8, name + "_scales")
+            per = K_PASS // len(engines)
+            for h, engine in enumerate(engines):
+                cols = slice(h * per, (h + 1) * per)
+                grouped = ring.tile([P, per, PACK], BF16, name="grouped", align_bytes=64)
+                neg_cast(engine, grouped[:].rearrange("p (c e) i -> p c i e", e=4),
+                         raw[:, :, cols].rearrange("p i (c e) -> p c i e", e=4), 1.0)
+                quantise(grouped[:].rearrange("p c i -> p (c i)"), codes[:, cols], scales[:, cols])
+            return codes, scales
+
+        def tab_pass(words, a):
+            return words[a].rearrange("p t i -> p (t i)")
+
+        def passes(bank, lhsT, lhsT_scale, lhsT_fmt, rhs, rhs_scale, rhs_fmt, first, last):
+            for t in range(4):
+                nc.tensor.matmul_mx(
+                    out=bank[:, t, :], lhsT=lhsT(t).bitcast(lhsT_fmt), lhsT_scale=lhsT_scale(t),
+                    rhs=rhs.bitcast(rhs_fmt), rhs_scale=rhs_scale,
+                    start=first and t == 0, stop=last and t == 3)
+
+        d_banks = [[psum.tile([P, PACK, CHUNK], F32, name="bank%d" % (b * CHUNKS + c)) for c in range(CHUNKS)] for b in range(2)]
+
+        def bowl_passes(b, a, w2q, first, last):
+            codes, scales = w2q
+            for c in range(CHUNKS):
+                passes(d_banks[b][c],
+                       lambda t: codes[:, t * P:(t + 1) * P], lambda t: scales[:, t * P:(t + 1) * P], E4M3,
+                       v2_words[a][:, 4 * c * CHUNK:4 * (c + 1) * CHUNK], v2_sc[4 * (a + 1):P, c * CHUNK:(c + 1) * CHUNK], E4M3,
+                       first, last)
+
+        def bat_passes(b, a, first, last):
+            for c in range(CHUNKS):
+                passes(d_banks[b][c],
+                       lambda t: w1_perm[:, a, 2 * (b * K_PASS + t * P):2 * (b * K_PASS + (t + 1) * P)],
+                       lambda t: w1_sc[:, a, b * K_PASS + t * P:b * K_PASS + (t + 1) * P], E2M1,
+                       v_words[a][:, 4 * c * CHUNK:4 * (c + 1) * CHUNK], v_sc[a][:, c * CHUNK:(c + 1) * CHUNK], E4M3,
+                       first, last)
+
+        def surplus(b, c):
+            d = ring.tile([P, CHUNK, PACK], BF16, name="d", align_bytes=64)
+            nc.scalar.copy(d[:], d_banks[b][c][:].rearrange("p t j -> p j t"))
+            parts = ring.tile([P, 2, CHUNK * PACK], BF16, name="parts", align_bytes=64)
+            flat = d[:].rearrange("p j t -> p (j t)")
+            nc.vector.tensor_scalar(parts[:, 0, :], flat, 0.0, None, ALU.max)
+            nc.vector.tensor_scalar(parts[:, 1, :], flat, 0.0, None, ALU.min)
+            codes = held([P, 2 * CHUNK], U32, "h_codes%d%d" % (b, c))
+            scales = held([P, 2 * CHUNK], U8, "h_scales%d%d" % (b, c))
+            quantise(parts[:].rearrange("p s x -> p (s x)"), codes[:], scales[:])
+            return codes, scales
+
+        v2_words, v_words, v_sc = {}, {}, {}
+        S_ONLY, BOTH = ["scalar"], ["scalar", "vector"]
+
+        w4q = {}
+
+        def hp_passes(b, c, h, first, last):
+            codes, scales = w4q[b]
+            passes(out_banks[c], lambda t: codes[:, t * P:(t + 1) * P], lambda t: scales[:, t * P:(t + 1) * P], E4M3,
+                   h[0][:, 0:CHUNK], h[1][:, 0:CHUNK], E4M3, first, last)
+
+        def hn_passes(b, c, h, first, last):
+            passes(out_banks[c], lambda t: w5_sb[:, b, 2 * t * P:2 * (t + 1) * P], lambda t: w5_sc[:, b, t * P:(t + 1) * P], E2M1,
+                   h[0][:, CHUNK:2 * CHUNK], h[1][:, CHUNK:2 * CHUNK], E4M3, first, last)
+
+        def ground_passes(c, first, last):
+            passes(out_banks[c], lambda t: w3_sb[:, 4 * t * P:4 * (t + 1) * P], lambda t: w3_sc[:, 0, t * P:(t + 1) * P], E4M3,
+                   v3_words[:, 2 * c * CHUNK:2 * (c + 1) * CHUNK], v3_sc[:, c * CHUNK:(c + 1) * CHUNK], E2M1, first, last)
+
+        def finish(c, engine):
+            result = ring.tile([P, N_TILES, CHUNK], F32, name="result")
+            if engine == "S":
+                nc.scalar.copy(result[:], out_banks[c][:])
+            else:
+                nc.vector.tensor_copy(result[:], out_banks[c][:])
+            nc.sync.dma_start(out[:, c * CHUNK:(c + 1) * CHUNK].rearrange("(t p) j -> p t j", p=P), result[:])
+
+        list2 = load_list(offs2, "list2")
+        list1 = load_list(offs, "list1")
+        list3 = load_list(offs3, "list3")
+        w1_raw = [load_bytes(w1_words[a], "w1_raw%d" % a) for a in range(2)]
+        u0 = load_bytes(tab_pass(tab2_words, 0), "tab2_w0")
+        for q in range(4):
+            nc.sync.dma_start(tab2_sc[32 * q + 4:32 * q + 16, :].bitcast(I32), tab2_scales[:, 4 * q:4 * q + 4, :].bitcast(I32))
+        t3 = load_bytes(tab3_words[0], "tab3_w")
+        x00 = load_w2(0, 0)
+        t0 = load_bytes(tab_pass(tab_words, 0), "tab_w0")
+        load_scales(w1_sc_raw, w1_scales)
+        u1 = load_bytes(tab_pass(tab2_words, 1), "tab2_w1")
+        load_scales(tab_sc, tab_scales)
+        x10 = load_w2(1, 0)
+        load_scales(tab3_sc, tab3_scales)
+        t1 = load_bytes(tab_pass(tab_words, 1), "tab_w1")
+        load_scales(w5_sc, w5_scales)
+        u2 = load_bytes(tab_pass(tab2_words, 2), "tab2_w2")
+        load_scales(w3_sc, w3_scales)
+        x20 = load_w2(2, 0)
+        w5_sb = held([P, 2, 1024], U8, "w5_sb")
+        nc.sync.dma_start(w5_sb[:].bitcast(I32), w5_words.rearrange("a p c -> p a c").bitcast(I32))
+        w3_sb = load_bytes(tab_pass(w3_words, 0), "w3_sb")
+        x01 = load_w2(0, 1)
+        x11 = load_w2(1, 1)
+        x21 = load_w2(2, 1)
+        y0 = load_w4(0)
+        y1 = load_w4(1)
+
+        w1_perm = held([P, 2, 2048], U8, "w1_perm")
+        for a in range(2):
+            nc.vector.tensor_copy(w1_perm[:, a, :].bitcast(U16).rearrange("p (b t m) -> p b t m", t=PACK, m=P),
+                                  w1_raw[a][:].bitcast(U16).rearrange("p (b m t) -> p b t m", t=PACK, m=P))
+        v2_words[0] = gather(u0[:], list2, U32, "v2_w0")
+        v2_sc = gather(tab2_sc[:], list2, U8, "v2_sc")
+        q00 = quantise_w2(x00, S_ONLY, "w2q00")
+        bowl_passes(0, 0, q00, True, False)
+        w1_sc = held([P, 2, 1024], U8, "w1_sc")
+        nc.vector.tensor_copy(w1_sc[:].rearrange("p a (b t m) -> p (a b) t m", t=PACK, m=P),
+                              w1_sc_raw[:].rearrange("p a (b m t) -> p (a b) t m", t=PACK, m=P))
+        v_words[0] = gather(t0[:], list1, U32, "v_w0")
+        v_sc[0] = gather(tab_sc[:, 0, :], list1, U8, "v_sc0")
+        bat_passes(0, 0, False, False)
+        v2_words[1] = gather(u1[:], list2, U32, "v2_w1")
+        q10 = quantise_w2(x10, S_ONLY, "w2q10")
+        bowl_passes(0, 1, q10, False, False)
+        v_sc[1] = gather(tab_sc[:, 1, :], list1, U8, "v_sc1")
+        v_words[1] = gather(t1[:], list1, U32, "v_w1")
+        bat_passes(0, 1, False, False)
+        v2_words[2] = gather(u2[:], list2, U32, "v2_w2")
+        q20 = quantise_w2(x20, BOTH, "w2q20")
+        bowl_passes(0, 2, q20, False, True)
+        bat_passes(1, 0, True, False)
+        bat_passes(1, 1, False, False)
+        v3_words = gather(t3[:], list3, U16, "v3_w")
+        v3_sc = gather(tab3_sc[:, 0, :], list3, U8, "v3_sc")
+        h0 = [surplus(0, c) for c in range(CHUNKS)]
+        q01 = quantise_w2(x01, ["scalar", "scalar"], "w2q01")
+        bowl_passes(1, 0, q01, False, False)
+        q11 = quantise_w2(x11, BOTH, "w2q11")
+        bowl_passes(1, 1, q11, False, False)
+        q21 = quantise_w2(x21, BOTH, "w2q21")
+        bowl_passes(1, 2, q21, False, True)
+        out_banks = [psum.tile([P, N_TILES, CHUNK], F32, name="bank%d" % c) for c in range(CHUNKS)]
+        for c in range(CHUNKS):
+            hn_passes(0, c, h0[c], True, False)
+        for c in range(CHUNKS):
+            ground_passes(c, False, False)
+        w4q[0] = quantise_w4(y0, BOTH, "w4q0")
+        w4q[1] = quantise_w4(y1, BOTH, "w4q1")
+        h1 = [surplus(1, c) for c in range(CHUNKS)]
+        for c in range(CHUNKS):
+            hp_passes(0, c, h0[c], False, False)
+        for c in range(CHUNKS):
+            hn_passes(1, c, h1[c], False, False)
+            hp_passes(1, c, h1[c], False, True)
+            finish(c, "SSSV"[c])

@@ -41,12 +41,13 @@ def tile_list_fixture_surplus_scores_kernel(
             engine.memset(tile[:].bitcast(I32), 0)
             return tile
 
+        tab_sc = zeroed([P, 2048], "tab_sc", nc.gpsimd)
         tab2_sc = zeroed([P, 2048], "tab2_sc", nc.gpsimd)
         w1_sc_raw = zeroed([P, 2, 1024], "w1_sc_raw", nc.vector)
-        tab_sc = zeroed([P, 2, 2048], "tab_sc", nc.vector)
-        tab3_sc = zeroed([P, 1, 1024], "tab3_sc", nc.gpsimd)
-        w5_sc = zeroed([P, 2, 512], "w5_sc", nc.gpsimd)
-        w3_sc = zeroed([P, 1, 512], "w3_sc", nc.gpsimd)
+        v_sc_planes = zeroed([P, 2, S], "v_sc_planes", nc.vector)
+        tab3_sc = zeroed([P, 1, 1024], "tab3_sc", nc.vector)
+        w5_sc = zeroed([P, 2, 512], "w5_sc", nc.vector)
+        w3_sc = zeroed([P, 1, 512], "w3_sc", nc.vector)
 
         def load_list(src, name):
             tile = keep.tile([P, S // 16], U16, name=name)
@@ -58,10 +59,10 @@ def tile_list_fixture_surplus_scores_kernel(
             nc.sync.dma_start(tile[:].bitcast(I32), src.bitcast(I32))
             return tile
 
-        def load_scales(tile, src):
+        def load_scales(tile, src, queue):
             rows = src.rearrange("a (q r) c -> r q a c", r=4)
             for r in range(4):
-                nc.sync.dma_start(tile[r:P:32, :, :].bitcast(I32), rows[r].bitcast(I32))
+                queue.dma_start(tile[r:P:32, :, :].bitcast(I32), rows[r].bitcast(I32))
 
         def load_w2(a, b):
             tile = held([P, PACK, K_PASS], F32, "w2_raw%d%d" % (a, b))
@@ -93,10 +94,13 @@ def tile_list_fixture_surplus_scores_kernel(
             codes = held([P, K_PASS], U32, name + "_codes")
             scales = held([P, K_PASS], U8, name + "_scales")
             per = PACK // len(engines)
+            staged = []
             for h, engine in enumerate(engines):
                 grouped = ring.tile([P, per, P, PACK], BF16, name="grouped", align_bytes=64)
+                staged.append(grouped)
                 src = raw[:].rearrange("p i (m t) -> p m i t", t=PACK)[:, :, :, h * per:(h + 1) * per]
                 neg_cast(engine, grouped[:].rearrange("p t m i -> p m i t"), src, -1.0)
+            for h, grouped in enumerate(staged):
                 cols = slice(h * per * P, (h + 1) * per * P)
                 quantise(grouped[:].rearrange("p t m i -> p (t m i)"), codes[:, cols], scales[:, cols])
             return codes, scales
@@ -105,11 +109,15 @@ def tile_list_fixture_surplus_scores_kernel(
             codes = held([P, K_PASS], U32, name + "_codes")
             scales = held([P, K_PASS], U8, name + "_scales")
             per = K_PASS // len(engines)
+            staged = []
             for h, engine in enumerate(engines):
                 cols = slice(h * per, (h + 1) * per)
                 grouped = ring.tile([P, per, PACK], BF16, name="grouped", align_bytes=64)
+                staged.append(grouped)
                 neg_cast(engine, grouped[:].rearrange("p (c e) i -> p c i e", e=4),
                          raw[:, :, cols].rearrange("p i (c e) -> p c i e", e=4), 1.0)
+            for h, grouped in enumerate(staged):
+                cols = slice(h * per, (h + 1) * per)
                 quantise(grouped[:].rearrange("p c i -> p (c i)"), codes[:, cols], scales[:, cols])
             return codes, scales
 
@@ -154,7 +162,7 @@ def tile_list_fixture_surplus_scores_kernel(
             return codes, scales
 
         v2_words, v_words, v_sc = {}, {}, {}
-        S_ONLY, BOTH = ["scalar"], ["scalar", "vector"]
+        S_ONLY, BOTH = ["scalar"], ["vector", "scalar"]
 
         w4q = {}
 
@@ -179,79 +187,83 @@ def tile_list_fixture_surplus_scores_kernel(
                 nc.vector.tensor_copy(result[:], out_banks[c][:])
             nc.sync.dma_start(out[:, c * CHUNK:(c + 1) * CHUNK].rearrange("(t p) j -> p t j", p=P), result[:])
 
-        list2 = load_list(offs2, "list2")
-        list1 = load_list(offs, "list1")
-        list3 = load_list(offs3, "list3")
-        w1_raw = [load_bytes(w1_words[a], "w1_raw%d" % a) for a in range(2)]
-        u0 = load_bytes(tab_pass(tab2_words, 0), "tab2_w0")
         for q in range(4):
-            nc.sync.dma_start(tab2_sc[32 * q + 4:32 * q + 16, :].bitcast(I32), tab2_scales[:, 4 * q:4 * q + 4, :].bitcast(I32))
-        t3 = load_bytes(tab3_words[0], "tab3_w")
-        x00 = load_w2(0, 0)
+            nc.gpsimd.dma_start(tab2_sc[32 * q + 4:32 * q + 16, :].bitcast(I32), tab2_scales[:, 4 * q:4 * q + 4, :].bitcast(I32))
+        list1 = load_list(offs, "list1")
+        list2 = load_list(offs2, "list2")
+        nc.sync.dma_start(tab_sc[0:32, :].bitcast(I32), tab_scales.rearrange("a q c -> (a q) c").bitcast(I32))
         t0 = load_bytes(tab_pass(tab_words, 0), "tab_w0")
-        load_scales(w1_sc_raw, w1_scales)
-        u1 = load_bytes(tab_pass(tab2_words, 1), "tab2_w1")
-        load_scales(tab_sc, tab_scales)
-        x10 = load_w2(1, 0)
-        load_scales(tab3_sc, tab3_scales)
+        w1_raw = [load_bytes(w1_words[a], "w1_raw%d" % a) for a in range(2)]
+        x00 = load_w2(0, 0)
+        u0 = load_bytes(tab_pass(tab2_words, 0), "tab2_w0")
+        v_sc_rows = gather(tab_sc[:], list1, U8, "v_sc_rows")
+        load_scales(w1_sc_raw, w1_scales, nc.sync)
         t1 = load_bytes(tab_pass(tab_words, 1), "tab_w1")
-        load_scales(w5_sc, w5_scales)
+        for r in range(4):
+            nc.sync.dma_start(v_sc_planes[r:P:32, 0, :].bitcast(I32), v_sc_rows[16 * 0 + r:16 * (0 + 1):4, :].bitcast(I32))
+        v_sc[0] = v_sc_planes[:, 0, :]
+        x10 = load_w2(1, 0)
+        for r in range(4):
+            nc.sync.dma_start(v_sc_planes[r:P:32, 1, :].bitcast(I32), v_sc_rows[16 * 1 + r:16 * (1 + 1):4, :].bitcast(I32))
+        v_sc[1] = v_sc_planes[:, 1, :]
+        u1 = load_bytes(tab_pass(tab2_words, 1), "tab2_w1")
+        list3 = load_list(offs3, "list3")
+        load_scales(tab3_sc, tab3_scales, nc.sync)
+        t3 = load_bytes(tab3_words[0], "tab3_w")
         u2 = load_bytes(tab_pass(tab2_words, 2), "tab2_w2")
-        load_scales(w3_sc, w3_scales)
         x20 = load_w2(2, 0)
+        x01 = load_w2(0, 1)
+        load_scales(w5_sc, w5_scales, nc.sync)
         w5_sb = held([P, 2, 1024], U8, "w5_sb")
         nc.sync.dma_start(w5_sb[:].bitcast(I32), w5_words.rearrange("a p c -> p a c").bitcast(I32))
-        w3_sb = load_bytes(tab_pass(w3_words, 0), "w3_sb")
-        x01 = load_w2(0, 1)
         x11 = load_w2(1, 1)
         x21 = load_w2(2, 1)
         y0 = load_w4(0)
         y1 = load_w4(1)
-
+        load_scales(w3_sc, w3_scales, nc.sync)
+        w3_sb = load_bytes(tab_pass(w3_words, 0), "w3_sb")
         w1_perm = held([P, 2, 2048], U8, "w1_perm")
         for a in range(2):
             nc.vector.tensor_copy(w1_perm[:, a, :].bitcast(U16).rearrange("p (b t m) -> p b t m", t=PACK, m=P),
                                   w1_raw[a][:].bitcast(U16).rearrange("p (b m t) -> p b t m", t=PACK, m=P))
-        v2_words[0] = gather(u0[:], list2, U32, "v2_w0")
-        v2_sc = gather(tab2_sc[:], list2, U8, "v2_sc")
-        q00 = quantise_w2(x00, S_ONLY, "w2q00")
-        bowl_passes(0, 0, q00, True, False)
+        v_words[0] = gather(t0[:], list1, U32, "v_w0")
         w1_sc = held([P, 2, 1024], U8, "w1_sc")
         nc.vector.tensor_copy(w1_sc[:].rearrange("p a (b t m) -> p (a b) t m", t=PACK, m=P),
                               w1_sc_raw[:].rearrange("p a (b m t) -> p (a b) t m", t=PACK, m=P))
-        v_words[0] = gather(t0[:], list1, U32, "v_w0")
-        v_sc[0] = gather(tab_sc[:, 0, :], list1, U8, "v_sc0")
-        bat_passes(0, 0, False, False)
-        v2_words[1] = gather(u1[:], list2, U32, "v2_w1")
-        q10 = quantise_w2(x10, S_ONLY, "w2q10")
-        bowl_passes(0, 1, q10, False, False)
-        v_sc[1] = gather(tab_sc[:, 1, :], list1, U8, "v_sc1")
+        bat_passes(0, 0, True, False)
+        bat_passes(1, 0, True, False)
         v_words[1] = gather(t1[:], list1, U32, "v_w1")
         bat_passes(0, 1, False, False)
+        bat_passes(1, 1, False, False)
+        q00 = quantise_w2(x00, S_ONLY, "w2q00")
+        v2_words[0] = gather(u0[:], list2, U32, "v2_w0")
+        v2_sc = gather(tab2_sc[:], list2, U8, "v2_sc")
+        bowl_passes(0, 0, q00, False, False)
+        q10 = quantise_w2(x10, S_ONLY, "w2q10")
+        v2_words[1] = gather(u1[:], list2, U32, "v2_w1")
+        bowl_passes(0, 1, q10, False, False)
         v2_words[2] = gather(u2[:], list2, U32, "v2_w2")
         q20 = quantise_w2(x20, BOTH, "w2q20")
         bowl_passes(0, 2, q20, False, True)
-        bat_passes(1, 0, True, False)
-        bat_passes(1, 1, False, False)
         v3_words = gather(t3[:], list3, U16, "v3_w")
         v3_sc = gather(tab3_sc[:, 0, :], list3, U8, "v3_sc")
-        h0 = [surplus(0, c) for c in range(CHUNKS)]
-        q01 = quantise_w2(x01, ["scalar", "scalar"], "w2q01")
+        q01 = quantise_w2(x01, BOTH, "w2q01")
         bowl_passes(1, 0, q01, False, False)
         q11 = quantise_w2(x11, BOTH, "w2q11")
         bowl_passes(1, 1, q11, False, False)
         q21 = quantise_w2(x21, BOTH, "w2q21")
         bowl_passes(1, 2, q21, False, True)
+        h0 = [surplus(0, c) for c in range(CHUNKS)]
         out_banks = [psum.tile([P, N_TILES, CHUNK], F32, name="bank%d" % c) for c in range(CHUNKS)]
         for c in range(CHUNKS):
             hn_passes(0, c, h0[c], True, False)
-        for c in range(CHUNKS):
-            ground_passes(c, False, False)
         w4q[0] = quantise_w4(y0, BOTH, "w4q0")
         w4q[1] = quantise_w4(y1, BOTH, "w4q1")
         h1 = [surplus(1, c) for c in range(CHUNKS)]
         for c in range(CHUNKS):
             hp_passes(0, c, h0[c], False, False)
+        for c in range(CHUNKS):
+            ground_passes(c, False, False)
         for c in range(CHUNKS):
             hn_passes(1, c, h1[c], False, False)
             hp_passes(1, c, h1[c], False, True)

@@ -22,6 +22,8 @@ CHUNKS = S // CHUNK
 N_TILES = 4
 FLOPS = 2 * S * (1024 * 1024 + 1536 * 1024 + 2 * 1024 * 512 + 512 * 512)
 
+W3_AT, W5_AT, SLOT = 512, 640, 896
+
 
 def tile_list_fixture_surplus_scores_kernel(
     tc, tab_words, tab_scales, tab2_words, tab2_scales, tab3_words, tab3_scales, offs, offs2, offs3,
@@ -33,21 +35,21 @@ def tile_list_fixture_surplus_scores_kernel(
         ring = ctx.enter_context(tc.tile_pool(name="ring", bufs=4))
         psum = ctx.enter_context(tc.psum_pool(name="psum", bufs=1))
 
-        def held(shape, dtype, name):
-            return keep.tile(shape, dtype, name=name, align_bytes=64)
+        def held(shape, dtype, name, tag=None):
+            return keep.tile(shape, dtype, name=name, tag=tag or name, align_bytes=64)
 
         def zeroed(shape, name, engine):
             tile = held(shape, U8, name)
             engine.memset(tile[:].bitcast(I32), 0)
             return tile
 
+        w1_sc_raw = zeroed([P, 512], "w1_sc_raw", nc.gpsimd)
         tab_sc = zeroed([P, 2048], "tab_sc", nc.gpsimd)
-        tab2_sc = zeroed([P, 2048], "tab2_sc", nc.gpsimd)
-        w1_sc_raw = zeroed([P, 2, 1024], "w1_sc_raw", nc.vector)
-        v_sc_planes = zeroed([P, 2, S], "v_sc_planes", nc.vector)
-        tab3_sc = zeroed([P, 1, 1024], "tab3_sc", nc.vector)
-        w5_sc = zeroed([P, 2, 512], "w5_sc", nc.vector)
-        w3_sc = zeroed([P, 1, 512], "w3_sc", nc.vector)
+        tab2_sc = zeroed([P, 2048], "tab2_sc", nc.vector)
+        tab3_sc = zeroed([P, 1024], "tab3_sc", nc.vector)
+        w_planes = zeroed([P, 4, SLOT], "w_planes", nc.vector)
+        v_planes = zeroed([P, 2, S], "v_planes", nc.vector)
+        staged_sc = held([P, SLOT], U8, "staged_sc")
 
         def load_list(src, name):
             tile = keep.tile([P, S // 16], U16, name=name)
@@ -59,30 +61,33 @@ def tile_list_fixture_surplus_scores_kernel(
             nc.sync.dma_start(tile[:].bitcast(I32), src.bitcast(I32))
             return tile
 
-        def load_scales(tile, src, queue):
-            rows = src.rearrange("a (q r) c -> r q a c", r=4)
-            for r in range(4):
-                queue.dma_start(tile[r:P:32, :, :].bitcast(I32), rows[r].bitcast(I32))
+        def load_passes(src, name, tag=None):
+            tile = held([P, src.shape[0], src.shape[2]], U8, name, tag)
+            nc.sync.dma_start(tile[:].bitcast(I32), src.rearrange("a p c -> p a c").bitcast(I32))
+            return tile
+
+        def load_spread(dst, src):
+            nc.sync.dma_start(dst.bitcast(I32), src.bitcast(I32))
+
+        def load_rows(src, name):
+            tile = held([P, PACK, src.shape[1]], F32, name)
+            nc.sync.dma_start(tile[:], src.rearrange("(p i) c -> p i c", i=PACK))
+            return tile
 
         def load_w2(a, b):
-            tile = held([P, PACK, K_PASS], F32, "w2_raw%d%d" % (a, b))
-            rows = w2[a * K_PASS:(a + 1) * K_PASS, b * K_PASS:(b + 1) * K_PASS]
-            nc.sync.dma_start(tile[:], rows.rearrange("(p i) c -> p i c", i=PACK))
-            return tile
+            return load_rows(w2[a * K_PASS:(a + 1) * K_PASS, b * K_PASS:(b + 1) * K_PASS], "w2_raw%d%d" % (a, b))
 
-        def load_w4(b):
-            tile = held([P, PACK, K_PASS], F32, "w4_raw%d" % b)
-            nc.sync.dma_start(tile[:], w4[b * K_PASS:(b + 1) * K_PASS, :].rearrange("(p i) c -> p i c", i=PACK))
-            return tile
+        def gather_into(dst, window, offsets, dtype):
+            nc.vector.tensor_copy(dst.bitcast(dtype), window.bitcast(dtype).indirect(offsets[:]))
 
-        def gather(window, offsets, dtype, name):
+        def gather(window, offsets, dtype, name, tag=None):
             width = {U32: 4, U16: 2, U8: 1}[dtype]
-            tile = held([P, S * width], U8, name)
-            nc.vector.tensor_copy(tile[:].bitcast(dtype), window.bitcast(dtype).indirect(offsets[:]))
+            tile = held([P, S * width], U8, name, tag)
+            gather_into(tile[:], window, offsets, dtype)
             return tile
 
-        def neg_cast(engine, dst, src, factor):
-            if engine == "scalar":
+        def cast(engine, dst, src, factor):
+            if engine == "S":
                 nc.scalar.activation(dst, src, ACT.Copy, scale=factor)
             else:
                 nc.vector.tensor_scalar(dst, src, factor, None, ALU.mult)
@@ -90,181 +95,189 @@ def tile_list_fixture_surplus_scores_kernel(
         def quantise(grouped, codes, scales):
             nc.vector.quantize_mx(out=codes.bitcast(E4M3), scales=scales, in_=grouped)
 
-        def quantise_w2(raw, engines, name):
+        def quantise_w2(raw, engines, tags, name):
             codes = held([P, K_PASS], U32, name + "_codes")
             scales = held([P, K_PASS], U8, name + "_scales")
-            per = PACK // len(engines)
-            staged = []
+            if len(tags) == 1:
+                whole = held([P, PACK, P, PACK], BF16, name + "_grouped", tags[0])
+                staged = [whole[:, 0:2, :, :], whole[:, 2:4, :, :]]
+            else:
+                staged = [held([P, 2, P, PACK], BF16, name + "_grouped%d" % h, tags[h])[:] for h in range(2)]
             for h, engine in enumerate(engines):
-                grouped = ring.tile([P, per, P, PACK], BF16, name="grouped", align_bytes=64)
-                staged.append(grouped)
-                src = raw[:].rearrange("p i (m t) -> p m i t", t=PACK)[:, :, :, h * per:(h + 1) * per]
-                neg_cast(engine, grouped[:].rearrange("p t m i -> p m i t"), src, -1.0)
+                src = raw[:].rearrange("p i (m t) -> p m i t", t=PACK)[:, :, :, 2 * h:2 * h + 2]
+                cast(engine, staged[h].rearrange("p t m i -> p m i t"), src, -1.0)
             for h, grouped in enumerate(staged):
-                cols = slice(h * per * P, (h + 1) * per * P)
-                quantise(grouped[:].rearrange("p t m i -> p (t m i)"), codes[:, cols], scales[:, cols])
-            return codes, scales
-
-        def quantise_w4(raw, engines, name):
-            codes = held([P, K_PASS], U32, name + "_codes")
-            scales = held([P, K_PASS], U8, name + "_scales")
-            per = K_PASS // len(engines)
-            staged = []
-            for h, engine in enumerate(engines):
-                cols = slice(h * per, (h + 1) * per)
-                grouped = ring.tile([P, per, PACK], BF16, name="grouped", align_bytes=64)
-                staged.append(grouped)
-                neg_cast(engine, grouped[:].rearrange("p (c e) i -> p c i e", e=4),
-                         raw[:, :, cols].rearrange("p i (c e) -> p c i e", e=4), 1.0)
-            for h, grouped in enumerate(staged):
-                cols = slice(h * per, (h + 1) * per)
-                quantise(grouped[:].rearrange("p c i -> p (c i)"), codes[:, cols], scales[:, cols])
+                cols = slice(2 * h * P, 2 * (h + 1) * P)
+                quantise(grouped.rearrange("p t m i -> p (t m i)"), codes[:, cols], scales[:, cols])
             return codes, scales
 
         def tab_pass(words, a):
             return words[a].rearrange("p t i -> p (t i)")
 
-        def passes(bank, lhsT, lhsT_scale, lhsT_fmt, rhs, rhs_scale, rhs_fmt, first, last):
-            for t in range(4):
-                nc.tensor.matmul_mx(
-                    out=bank[:, t, :], lhsT=lhsT(t).bitcast(lhsT_fmt), lhsT_scale=lhsT_scale(t),
-                    rhs=rhs.bitcast(rhs_fmt), rhs_scale=rhs_scale,
-                    start=first and t == 0, stop=last and t == 3)
+        def mx(dst, lhsT, lhsT_scale, lhsT_fmt, rhs, rhs_scale, rhs_fmt, start, stop):
+            nc.tensor.matmul_mx(out=dst, lhsT=lhsT.bitcast(lhsT_fmt), lhsT_scale=lhsT_scale,
+                                rhs=rhs.bitcast(rhs_fmt), rhs_scale=rhs_scale, start=start, stop=stop)
 
         d_banks = [[psum.tile([P, PACK, CHUNK], F32, name="bank%d" % (b * CHUNKS + c)) for c in range(CHUNKS)] for b in range(2)]
 
         def bowl_passes(b, a, w2q, first, last):
             codes, scales = w2q
             for c in range(CHUNKS):
-                passes(d_banks[b][c],
-                       lambda t: codes[:, t * P:(t + 1) * P], lambda t: scales[:, t * P:(t + 1) * P], E4M3,
+                for t in range(PACK):
+                    mx(d_banks[b][c][:, t, :], codes[:, t * P:(t + 1) * P], scales[:, t * P:(t + 1) * P], E4M3,
                        v2_words[a][:, 4 * c * CHUNK:4 * (c + 1) * CHUNK], v2_sc[4 * (a + 1):P, c * CHUNK:(c + 1) * CHUNK], E4M3,
-                       first, last)
+                       first and t == 0, last and t == PACK - 1)
 
         def bat_passes(b, a, first, last):
             for c in range(CHUNKS):
-                passes(d_banks[b][c],
-                       lambda t: w1_perm[:, a, 2 * (b * K_PASS + t * P):2 * (b * K_PASS + (t + 1) * P)],
-                       lambda t: w1_sc[:, a, b * K_PASS + t * P:b * K_PASS + (t + 1) * P], E2M1,
-                       v_words[a][:, 4 * c * CHUNK:4 * (c + 1) * CHUNK], v_sc[a][:, c * CHUNK:(c + 1) * CHUNK], E4M3,
-                       first, last)
+                for t in range(PACK):
+                    col = b * K_PASS + t * P
+                    mx(d_banks[b][c][:, t, :], w1_perm[:, a, 2 * col:2 * (col + P)],
+                       w_planes[:, 2 * b + a, t * P:(t + 1) * P], E2M1,
+                       v_words[a][:, 4 * c * CHUNK:4 * (c + 1) * CHUNK],
+                       v_planes[:, a, c * CHUNK:(c + 1) * CHUNK], E4M3,
+                       first and t == 0, last and t == PACK - 1)
 
-        def surplus(b, c):
-            d = ring.tile([P, CHUNK, PACK], BF16, name="d", align_bytes=64)
-            nc.scalar.copy(d[:], d_banks[b][c][:].rearrange("p t j -> p j t"))
-            parts = ring.tile([P, 2, CHUNK * PACK], BF16, name="parts", align_bytes=64)
-            flat = d[:].rearrange("p j t -> p (j t)")
-            nc.vector.tensor_scalar(parts[:, 0, :], flat, 0.0, None, ALU.max)
-            nc.vector.tensor_scalar(parts[:, 1, :], flat, 0.0, None, ALU.min)
-            codes = held([P, 2 * CHUNK], U32, "h_codes%d%d" % (b, c))
-            scales = held([P, 2 * CHUNK], U8, "h_scales%d%d" % (b, c))
-            quantise(parts[:].rearrange("p s x -> p (s x)"), codes[:], scales[:])
-            return codes, scales
+        def surplus(b, group):
+            parts_q = [(held([P, S], U32, "h_codes%d%d" % (b, s)), held([P, S], U8, "h_scales%d%d" % (b, s))) for s in range(2)]
+            for c0 in range(0, CHUNKS, group):
+                d = held([P, group, CHUNK, PACK], BF16, "d%d%d" % (b, c0))
+                for g in range(group):
+                    nc.scalar.copy(d[:, g, :, :], d_banks[b][c0 + g][:].rearrange("p t j -> p j t"))
+                flat = d[:].rearrange("p g j t -> p (g j t)")
+                parts = []
+                for s, op in enumerate((ALU.max, ALU.min)):
+                    part = held([P, group * CHUNK * PACK], BF16, "part%d%d%d" % (b, c0, s))
+                    nc.vector.tensor_scalar(part[:], flat, 0.0, None, op)
+                    parts.append(part)
+                cols = slice(c0 * CHUNK, (c0 + group) * CHUNK)
+                for s in range(2):
+                    quantise(parts[s][:], parts_q[s][0][:, cols], parts_q[s][1][:, cols])
+            return parts_q
 
-        v2_words, v_words, v_sc = {}, {}, {}
-        S_ONLY, BOTH = ["scalar"], ["vector", "scalar"]
-
-        w4q = {}
-
-        def hp_passes(b, c, h, first, last):
+        def hp_pass(b, n, j0, width, first, last):
             codes, scales = w4q[b]
-            passes(out_banks[c], lambda t: codes[:, t * P:(t + 1) * P], lambda t: scales[:, t * P:(t + 1) * P], E4M3,
-                   h[0][:, 0:CHUNK], h[1][:, 0:CHUNK], E4M3, first, last)
+            cols = slice(j0, j0 + width)
+            mx(out_banks[n][:, cols], codes[:, n * P:(n + 1) * P], scales[:, n * P:(n + 1) * P], E4M3,
+               h[b][0][0][:, cols], h[b][0][1][:, cols], E4M3, first, last)
 
-        def hn_passes(b, c, h, first, last):
-            passes(out_banks[c], lambda t: w5_sb[:, b, 2 * t * P:2 * (t + 1) * P], lambda t: w5_sc[:, b, t * P:(t + 1) * P], E2M1,
-                   h[0][:, CHUNK:2 * CHUNK], h[1][:, CHUNK:2 * CHUNK], E4M3, first, last)
+        def hn_pass(b, n, j0, width):
+            at = W5_AT + P * b
+            cols = slice(j0, j0 + width)
+            mx(out_banks[n][:, cols], w5_sb[:, b, 2 * n * P:2 * (n + 1) * P], w_planes[:, n, at:at + P], E2M1,
+               h[b][1][0][:, cols], h[b][1][1][:, cols], E4M3, False, False)
 
-        def ground_passes(c, first, last):
-            passes(out_banks[c], lambda t: w3_sb[:, 4 * t * P:4 * (t + 1) * P], lambda t: w3_sc[:, 0, t * P:(t + 1) * P], E4M3,
-                   v3_words[:, 2 * c * CHUNK:2 * (c + 1) * CHUNK], v3_sc[:, c * CHUNK:(c + 1) * CHUNK], E2M1, first, last)
+        def ground_pass(n, first, last):
+            mx(out_banks[n][:], w3_sb[:, 4 * n * P:4 * (n + 1) * P], w_planes[:, n, W3_AT:W5_AT], E4M3,
+               v3_words[:], v3_sc[:], E2M1, first, last)
 
-        def finish(c, engine):
-            result = ring.tile([P, N_TILES, CHUNK], F32, name="result")
+        def finish(n, engine):
+            result = ring.tile([P, S], F32, name="result")
             if engine == "S":
-                nc.scalar.copy(result[:], out_banks[c][:])
+                nc.scalar.copy(result[:], out_banks[n][:])
             else:
-                nc.vector.tensor_copy(result[:], out_banks[c][:])
-            nc.sync.dma_start(out[:, c * CHUNK:(c + 1) * CHUNK].rearrange("(t p) j -> p t j", p=P), result[:])
+                nc.vector.tensor_copy(result[:], out_banks[n][:])
+            nc.sync.dma_start(out[n * P:(n + 1) * P, :], result[:])
+
+        v2_words, h = {}, {}
 
         for q in range(4):
             nc.gpsimd.dma_start(tab2_sc[32 * q + 4:32 * q + 16, :].bitcast(I32), tab2_scales[:, 4 * q:4 * q + 4, :].bitcast(I32))
+        for r in range(4):
+            nc.gpsimd.dma_start(tab3_sc[r:P:32, :].bitcast(I32), tab3_scales[0, r:16:4, :].bitcast(I32))
+        w1_raw = load_passes(w1_words, "w1_raw")
         list1 = load_list(offs, "list1")
-        list2 = load_list(offs2, "list2")
-        nc.sync.dma_start(tab_sc[0:32, :].bitcast(I32), tab_scales.rearrange("a q c -> (a q) c").bitcast(I32))
-        t0 = load_bytes(tab_pass(tab_words, 0), "tab_w0")
-        w1_raw = [load_bytes(w1_words[a], "w1_raw%d" % a) for a in range(2)]
+        for a in range(2):
+            load_spread(w1_sc_raw[2 * a:P:4, :], w1_scales[a].rearrange("q (b c) -> (q b) c", b=2))
+        load_spread(tab_sc[0:P:4, :], tab_scales.rearrange("a q c -> q a c"))
         x00 = load_w2(0, 0)
         u0 = load_bytes(tab_pass(tab2_words, 0), "tab2_w0")
-        v_sc_rows = gather(tab_sc[:], list1, U8, "v_sc_rows")
-        load_scales(w1_sc_raw, w1_scales, nc.sync)
-        t1 = load_bytes(tab_pass(tab_words, 1), "tab_w1")
-        for r in range(4):
-            nc.sync.dma_start(v_sc_planes[r:P:32, 0, :].bitcast(I32), v_sc_rows[16 * 0 + r:16 * (0 + 1):4, :].bitcast(I32))
-        v_sc[0] = v_sc_planes[:, 0, :]
+        list2 = load_list(offs2, "list2")
+        load_spread(staged_sc[0:P:2, W3_AT:W5_AT], w3_scales[0].rearrange("q (n c) -> (q n) c", n=4))
+        for b in range(2):
+            load_spread(staged_sc[0:P:2, W5_AT + P * b:W5_AT + P * (b + 1)], w5_scales[b].rearrange("q (n c) -> (q n) c", n=4))
         x10 = load_w2(1, 0)
-        for r in range(4):
-            nc.sync.dma_start(v_sc_planes[r:P:32, 1, :].bitcast(I32), v_sc_rows[16 * 1 + r:16 * (1 + 1):4, :].bitcast(I32))
-        v_sc[1] = v_sc_planes[:, 1, :]
-        u1 = load_bytes(tab_pass(tab2_words, 1), "tab2_w1")
         list3 = load_list(offs3, "list3")
-        load_scales(tab3_sc, tab3_scales, nc.sync)
+        t0 = load_bytes(tab_pass(tab_words, 0), "tab_w0")
+        u1 = load_bytes(tab_pass(tab2_words, 1), "tab2_w1")
         t3 = load_bytes(tab3_words[0], "tab3_w")
-        u2 = load_bytes(tab_pass(tab2_words, 2), "tab2_w2")
         x20 = load_w2(2, 0)
+        u2 = load_bytes(tab_pass(tab2_words, 2), "tab2_w2")
+        t1 = load_bytes(tab_pass(tab_words, 1), "tab_w1")
         x01 = load_w2(0, 1)
-        load_scales(w5_sc, w5_scales, nc.sync)
-        w5_sb = held([P, 2, 1024], U8, "w5_sb")
-        nc.sync.dma_start(w5_sb[:].bitcast(I32), w5_words.rearrange("a p c -> p a c").bitcast(I32))
+        w3_sb = load_bytes(tab_pass(w3_words, 0), "w3_sb")
         x11 = load_w2(1, 1)
         x21 = load_w2(2, 1)
-        y0 = load_w4(0)
-        y1 = load_w4(1)
-        load_scales(w3_sc, w3_scales, nc.sync)
-        w3_sb = load_bytes(tab_pass(w3_words, 0), "w3_sb")
+        y0 = load_rows(w4[0:K_PASS, :], "w4_raw0")
+        y1 = [load_rows(w4[K_PASS:2 * K_PASS, 256 * u:256 * (u + 1)], "w4_raw1%d" % u) for u in range(2)]
+
         w1_perm = held([P, 2, 2048], U8, "w1_perm")
         for a in range(2):
             nc.vector.tensor_copy(w1_perm[:, a, :].bitcast(U16).rearrange("p (b t m) -> p b t m", t=PACK, m=P),
-                                  w1_raw[a][:].bitcast(U16).rearrange("p (b m t) -> p b t m", t=PACK, m=P))
-        v_words[0] = gather(t0[:], list1, U32, "v_w0")
-        w1_sc = held([P, 2, 1024], U8, "w1_sc")
-        nc.vector.tensor_copy(w1_sc[:].rearrange("p a (b t m) -> p (a b) t m", t=PACK, m=P),
-                              w1_sc_raw[:].rearrange("p a (b m t) -> p (a b) t m", t=PACK, m=P))
-        bat_passes(0, 0, True, False)
-        bat_passes(1, 0, True, False)
-        v_words[1] = gather(t1[:], list1, U32, "v_w1")
-        bat_passes(0, 1, False, False)
-        bat_passes(1, 1, False, False)
-        q00 = quantise_w2(x00, S_ONLY, "w2q00")
+                                  w1_raw[:, a, :].bitcast(U16).rearrange("p (b m t) -> p b t m", t=PACK, m=P))
+        nc.vector.tensor_copy(staged_sc[:, 0:W3_AT].rearrange("p (t m) -> p t m", t=PACK),
+                              w1_sc_raw[:].rearrange("p (m t) -> p t m", t=PACK))
+        v_sc_rows = gather(tab_sc[:], list1, U8, "v_sc_rows")
+        for q in range(4):
+            nc.gpsimd.dma_start(v_planes[32 * q:32 * q + 4, :, :].bitcast(I32), v_sc_rows[32 * q:32 * q + 32:4, :].bitcast(I32))
+        for q in range(4):
+            nc.gpsimd.dma_start(w_planes[32 * q:32 * q + 4, :, :].bitcast(I32), staged_sc[32 * q:32 * q + 32:2, :].bitcast(I32))
+        q00 = quantise_w2(x00, "SS", ["g00"], "w2q00")
         v2_words[0] = gather(u0[:], list2, U32, "v2_w0")
         v2_sc = gather(tab2_sc[:], list2, U8, "v2_sc")
-        bowl_passes(0, 0, q00, False, False)
-        q10 = quantise_w2(x10, S_ONLY, "w2q10")
-        v2_words[1] = gather(u1[:], list2, U32, "v2_w1")
+        v3_sc = gather(tab3_sc[:], list3, U8, "v3_sc")
+
+        v_words = {}
+        w4q = [(held([P, K_PASS], U32, "w4_codes%d" % b), held([P, K_PASS], U8, "w4_scales%d" % b)) for b in range(2)]
+
+        def w4_half(b, u, raw, engine, tag):
+            grouped = held([P, 256, PACK], BF16, "w4_grouped%d%d" % (b, u), tag)
+            cast(engine, grouped[:].rearrange("p (c e) i -> p c i e", e=4), raw.rearrange("p i (c e) -> p c i e", e=4), 1.0)
+            return grouped
+
+        def quantise_w4_half(b, u, grouped):
+            cols = slice(256 * u, 256 * (u + 1))
+            quantise(grouped[:].rearrange("p c i -> p (c i)"), w4q[b][0][:, cols], w4q[b][1][:, cols])
+
+        bowl_passes(0, 0, q00, True, False)
+        q10 = quantise_w2(x10, "SS", ["g10a", "g10b"], "w2q10")
+        v_words[0] = gather(t0[:], list1, U32, "v_w0", "g10a")
+        v2_words[1] = gather(u1[:], list2, U32, "v2_w1", "g10b")
         bowl_passes(0, 1, q10, False, False)
-        v2_words[2] = gather(u2[:], list2, U32, "v2_w2")
-        q20 = quantise_w2(x20, BOTH, "w2q20")
-        bowl_passes(0, 2, q20, False, True)
-        v3_words = gather(t3[:], list3, U16, "v3_w")
-        v3_sc = gather(tab3_sc[:, 0, :], list3, U8, "v3_sc")
-        q01 = quantise_w2(x01, BOTH, "w2q01")
+        bat_passes(0, 0, False, False)
+        bat_passes(1, 0, True, False)
+        v3_words = gather(t3[:], list3, U16, "v3_w", "tab2_w1")
+        q20 = quantise_w2(x20, "SS", ["g20"], "w2q20")
+        v2_words[2] = gather(u2[:], list2, U32, "v2_w2", "g20")
+        bowl_passes(0, 2, q20, False, False)
+        v_words[1] = gather(t1[:], list1, U32, "v_w1", "tab2_w2")
+        bat_passes(0, 1, False, True)
+        bat_passes(1, 1, False, False)
+        q01 = quantise_w2(x01, "VV", ["tab_w1"], "w2q01")
         bowl_passes(1, 0, q01, False, False)
-        q11 = quantise_w2(x11, BOTH, "w2q11")
+        h[0] = surplus(0, 2)
+        out_banks = [psum.tile([P, S], F32, name="bank%d" % n) for n in range(N_TILES)]
+        for n in range(N_TILES):
+            ground_pass(n, True, False)
+        q11 = quantise_w2(x11, "SS", ["d00"], "w2q11")
+        w5_sb = load_passes(w5_words, "w5_sb", "w2_raw11")
         bowl_passes(1, 1, q11, False, False)
-        q21 = quantise_w2(x21, BOTH, "w2q21")
+        q21 = quantise_w2(x21, "VS", ["part021", "d02"], "w2q21")
         bowl_passes(1, 2, q21, False, True)
-        h0 = [surplus(0, c) for c in range(CHUNKS)]
-        out_banks = [psum.tile([P, N_TILES, CHUNK], F32, name="bank%d" % c) for c in range(CHUNKS)]
-        for c in range(CHUNKS):
-            hn_passes(0, c, h0[c], True, False)
-        w4q[0] = quantise_w4(y0, BOTH, "w4q0")
-        w4q[1] = quantise_w4(y1, BOTH, "w4q1")
-        h1 = [surplus(1, c) for c in range(CHUNKS)]
-        for c in range(CHUNKS):
-            hp_passes(0, c, h0[c], False, False)
-        for c in range(CHUNKS):
-            ground_passes(c, False, False)
-        for c in range(CHUNKS):
-            hn_passes(1, c, h1[c], False, False)
-            hp_passes(1, c, h1[c], False, True)
-            finish(c, "SSSV"[c])
+        g0 = [w4_half(0, 0, y0[:, :, 0:256], "S", "d00"), w4_half(0, 1, y0[:, :, 256:512], "V", "d02")]
+        quantise_w4_half(0, 1, g0[1])
+        quantise_w4_half(0, 0, g0[0])
+        for n in range(N_TILES):
+            hp_pass(0, n, 0, S, False, False)
+        quantise_w4_half(1, 0, w4_half(1, 0, y1[0][:], "V", "d00"))
+        for n in range(N_TILES):
+            hn_pass(0, n, 0, S)
+        h[1] = surplus(1, 2)
+        quantise_w4_half(1, 1, w4_half(1, 1, y1[1][:], "S", "d10"))
+        for half in range(2):
+            for n in range(N_TILES):
+                for c in range(2):
+                    hn_pass(1, n, (2 * half + c) * CHUNK, CHUNK)
+        for n in range(N_TILES):
+            hp_pass(1, n, 0, S, False, True)
+            finish(n, "SVSV"[n])

@@ -22,7 +22,8 @@ CHUNKS = S // CHUNK
 N_TILES = 4
 FLOPS = 2 * S * (1024 * 1024 + 1536 * 1024 + 2 * 1024 * 512 + 512 * 512)
 
-W3_AT, W5_AT, SLOT = 512, 640, 896
+W1_AT, V_AT, FIRST_END = 0, 1024, 1536
+W5_AT, V3_AT, W3_AT, SECOND_END = 0, 1024, 1536, 2048
 
 
 def tile_list_fixture_surplus_scores_kernel(
@@ -43,21 +44,23 @@ def tile_list_fixture_surplus_scores_kernel(
             engine.memset(tile[:].bitcast(I32), 0)
             return tile
 
-        w1_sc_raw = zeroed([P, 512], "w1_sc_raw", nc.gpsimd)
+        w1_sc_raw = zeroed([P, 1024], "w1_sc_raw", nc.gpsimd)
         tab_sc = zeroed([P, 2048], "tab_sc", nc.gpsimd)
         tab2_sc = zeroed([P, 2048], "tab2_sc", nc.vector)
         tab3_sc = zeroed([P, 1024], "tab3_sc", nc.vector)
-        w_planes = zeroed([P, 4, SLOT], "w_planes", nc.vector)
-        v_planes = zeroed([P, 2, S], "v_planes", nc.vector)
-        staged_sc = held([P, SLOT], U8, "staged_sc")
+        planes0 = held([P, FIRST_END], U8, "planes0")
+        planes = [planes0, zeroed([P, FIRST_END], "planes1", nc.vector)]
+        planes2 = held([P, SECOND_END], U8, "planes2")
+        nc.vector.memset(planes2[:, W5_AT:V3_AT].bitcast(I32), 0)
+        nc.vector.memset(planes2[:, W3_AT:SECOND_END].bitcast(I32), 0)
 
         def load_list(src, name):
             tile = keep.tile([P, S // 16], U16, name=name)
             nc.sync.dma_start(tile[:], src)
             return tile
 
-        def load_bytes(src, name):
-            tile = held([P, src.shape[1]], U8, name)
+        def load_bytes(src, name, tag=None):
+            tile = held([P, src.shape[1]], U8, name, tag)
             nc.sync.dma_start(tile[:].bitcast(I32), src.bitcast(I32))
             return tile
 
@@ -67,15 +70,15 @@ def tile_list_fixture_surplus_scores_kernel(
             return tile
 
         def load_spread(dst, src):
-            nc.sync.dma_start(dst.bitcast(I32), src.bitcast(I32))
+            nc.sync.dma_start(dst.bitcast(I32), src.rearrange("a q c -> q a c").bitcast(I32))
 
-        def load_rows(src, name):
-            tile = held([P, PACK, src.shape[1]], F32, name)
+        def load_rows(src, name, tag=None):
+            tile = held([P, PACK, src.shape[1]], F32, name, tag)
             nc.sync.dma_start(tile[:], src.rearrange("(p i) c -> p i c", i=PACK))
             return tile
 
-        def load_w2(a, b):
-            return load_rows(w2[a * K_PASS:(a + 1) * K_PASS, b * K_PASS:(b + 1) * K_PASS], "w2_raw%d%d" % (a, b))
+        def load_w2(a):
+            return load_rows(w2[a * K_PASS:(a + 1) * K_PASS, :], "w2_raw%d" % a)
 
         def gather_into(dst, window, offsets, dtype):
             nc.vector.tensor_copy(dst.bitcast(dtype), window.bitcast(dtype).indirect(offsets[:]))
@@ -85,6 +88,15 @@ def tile_list_fixture_surplus_scores_kernel(
             tile = held([P, S * width], U8, name, tag)
             gather_into(tile[:], window, offsets, dtype)
             return tile
+
+        def gather_whole(window, offsets, name, tag=None):
+            tile = gather(window, offsets, U32, name, tag)
+            return [tile[:, 0:2 * S], tile[:, 2 * S:4 * S]]
+
+        def gather_half(window, offsets, half, name, tag=None):
+            tile = held([P, 2 * S], U8, name, tag)
+            nc.vector.tensor_copy(tile[:].bitcast(U32), window.bitcast(U32).indirect(offsets[:, 16 * half:16 * (half + 1)]))
+            return tile[:]
 
         def cast(engine, dst, src, factor):
             if engine == "S":
@@ -104,7 +116,7 @@ def tile_list_fixture_surplus_scores_kernel(
             else:
                 staged = [held([P, 2, P, PACK], BF16, name + "_grouped%d" % h, tags[h])[:] for h in range(2)]
             for h, engine in enumerate(engines):
-                src = raw[:].rearrange("p i (m t) -> p m i t", t=PACK)[:, :, :, 2 * h:2 * h + 2]
+                src = raw.rearrange("p i (m t) -> p m i t", t=PACK)[:, :, :, 2 * h:2 * h + 2]
                 cast(engine, staged[h].rearrange("p t m i -> p m i t"), src, -1.0)
             for h, grouped in enumerate(staged):
                 cols = slice(2 * h * P, 2 * (h + 1) * P)
@@ -120,40 +132,41 @@ def tile_list_fixture_surplus_scores_kernel(
 
         d_banks = [[psum.tile([P, PACK, CHUNK], F32, name="bank%d" % (b * CHUNKS + c)) for c in range(CHUNKS)] for b in range(2)]
 
-        def bowl_passes(b, a, w2q, first, last):
+        def bowl_chunk(b, a, c, w2q, first, last=False):
             codes, scales = w2q
-            for c in range(CHUNKS):
-                for t in range(PACK):
-                    mx(d_banks[b][c][:, t, :], codes[:, t * P:(t + 1) * P], scales[:, t * P:(t + 1) * P], E4M3,
-                       v2_words[a][:, 4 * c * CHUNK:4 * (c + 1) * CHUNK], v2_sc[4 * (a + 1):P, c * CHUNK:(c + 1) * CHUNK], E4M3,
-                       first and t == 0, last and t == PACK - 1)
+            for t in range(PACK):
+                mx(d_banks[b][c][:, t, :], codes[:, t * P:(t + 1) * P], scales[:, t * P:(t + 1) * P], E4M3,
+                   v2_words[a][c // 2][:, 4 * (c % 2) * CHUNK:4 * (c % 2 + 1) * CHUNK], v2_sc[4 * (a + 1):P, c * CHUNK:(c + 1) * CHUNK], E4M3,
+                   first and t == 0, last and t == PACK - 1)
 
-        def bat_passes(b, a, first, last):
-            for c in range(CHUNKS):
-                for t in range(PACK):
-                    col = b * K_PASS + t * P
-                    mx(d_banks[b][c][:, t, :], w1_perm[:, a, 2 * col:2 * (col + P)],
-                       w_planes[:, 2 * b + a, t * P:(t + 1) * P], E2M1,
-                       v_words[a][:, 4 * c * CHUNK:4 * (c + 1) * CHUNK],
-                       v_planes[:, a, c * CHUNK:(c + 1) * CHUNK], E4M3,
-                       first and t == 0, last and t == PACK - 1)
+        def bat_chunk(b, a, c, last):
+            for t in range(PACK):
+                col = b * K_PASS + t * P
+                mx(d_banks[b][c][:, t, :], w1_perm[:, a, 2 * col:2 * (col + P)],
+                   planes[a][:, W1_AT + col:W1_AT + col + P], E2M1,
+                   v_words[a][c // 2][:, 4 * (c % 2) * CHUNK:4 * (c % 2 + 1) * CHUNK],
+                   planes[a][:, V_AT + c * CHUNK:V_AT + (c + 1) * CHUNK], E4M3,
+                   False, last and t == PACK - 1)
 
-        def surplus(b, group):
-            parts_q = [(held([P, S], U32, "h_codes%d%d" % (b, s)), held([P, S], U8, "h_scales%d%d" % (b, s))) for s in range(2)]
-            for c0 in range(0, CHUNKS, group):
-                d = held([P, group, CHUNK, PACK], BF16, "d%d%d" % (b, c0))
-                for g in range(group):
-                    nc.scalar.copy(d[:, g, :, :], d_banks[b][c0 + g][:].rearrange("p t j -> p j t"))
-                flat = d[:].rearrange("p g j t -> p (g j t)")
-                parts = []
-                for s, op in enumerate((ALU.max, ALU.min)):
-                    part = held([P, group * CHUNK * PACK], BF16, "part%d%d%d" % (b, c0, s))
-                    nc.vector.tensor_scalar(part[:], flat, 0.0, None, op)
-                    parts.append(part)
-                cols = slice(c0 * CHUNK, (c0 + group) * CHUNK)
-                for s in range(2):
-                    quantise(parts[s][:], parts_q[s][0][:, cols], parts_q[s][1][:, cols])
-            return parts_q
+        h = [[(held([P, S], U32, "h_codes%d%d" % (b, s)), held([P, S], U8, "h_scales%d%d" % (b, s))) for s in range(2)]
+             for b in range(2)]
+
+        def evacuate(b, half):
+            d = held([P, 2, CHUNK, PACK], BF16, "d%d%d" % (b, half))
+            for g in range(2):
+                nc.scalar.copy(d[:, g, :, :], d_banks[b][2 * half + g][:].rearrange("p t j -> p j t"))
+            return d
+
+        def surplus(b, half, d, tag=None):
+            flat = d[:].rearrange("p g j t -> p (g j t)")
+            parts = []
+            for s, op in enumerate((ALU.max, ALU.min)):
+                part = held([P, 2 * CHUNK * PACK], BF16, "part%d%d%d" % (b, half, s), tag if s == 0 else None)
+                nc.vector.tensor_scalar(part[:], flat, 0.0, None, op)
+                parts.append(part)
+            cols = slice(2 * half * CHUNK, 2 * (half + 1) * CHUNK)
+            for s in range(2):
+                quantise(parts[s][:], h[b][s][0][:, cols], h[b][s][1][:, cols])
 
         def hp_pass(b, n, j0, width, first, last):
             codes, scales = w4q[b]
@@ -162,14 +175,14 @@ def tile_list_fixture_surplus_scores_kernel(
                h[b][0][0][:, cols], h[b][0][1][:, cols], E4M3, first, last)
 
         def hn_pass(b, n, j0, width):
-            at = W5_AT + P * b
+            at = W5_AT + b * K_PASS + n * P
             cols = slice(j0, j0 + width)
-            mx(out_banks[n][:, cols], w5_sb[:, b, 2 * n * P:2 * (n + 1) * P], w_planes[:, n, at:at + P], E2M1,
+            mx(out_banks[n][:, cols], w5_sb[:, b, 2 * n * P:2 * (n + 1) * P], planes2[:, at:at + P], E2M1,
                h[b][1][0][:, cols], h[b][1][1][:, cols], E4M3, False, False)
 
         def ground_pass(n, first, last):
-            mx(out_banks[n][:], w3_sb[:, 4 * n * P:4 * (n + 1) * P], w_planes[:, n, W3_AT:W5_AT], E4M3,
-               v3_words[:], v3_sc[:], E2M1, first, last)
+            mx(out_banks[n][:], w3_sb[:, 4 * n * P:4 * (n + 1) * P], planes2[:, W3_AT + n * P:W3_AT + (n + 1) * P], E4M3,
+               v3_words[:], planes2[:, V3_AT:V3_AT + S], E2M1, first, last)
 
         def finish(n, engine):
             result = ring.tile([P, S], F32, name="result")
@@ -179,53 +192,47 @@ def tile_list_fixture_surplus_scores_kernel(
                 nc.vector.tensor_copy(result[:], out_banks[n][:])
             nc.sync.dma_start(out[n * P:(n + 1) * P, :], result[:])
 
-        v2_words, h = {}, {}
+        v2_words = {}
 
         for q in range(4):
             nc.gpsimd.dma_start(tab2_sc[32 * q + 4:32 * q + 16, :].bitcast(I32), tab2_scales[:, 4 * q:4 * q + 4, :].bitcast(I32))
-        for r in range(4):
-            nc.gpsimd.dma_start(tab3_sc[r:P:32, :].bitcast(I32), tab3_scales[0, r:16:4, :].bitcast(I32))
         w1_raw = load_passes(w1_words, "w1_raw")
+        load_spread(w1_sc_raw[0:P:4, :], w1_scales)
         list1 = load_list(offs, "list1")
-        for a in range(2):
-            load_spread(w1_sc_raw[2 * a:P:4, :], w1_scales[a].rearrange("q (b c) -> (q b) c", b=2))
-        load_spread(tab_sc[0:P:4, :], tab_scales.rearrange("a q c -> q a c"))
-        x00 = load_w2(0, 0)
-        u0 = load_bytes(tab_pass(tab2_words, 0), "tab2_w0")
-        list2 = load_list(offs2, "list2")
-        load_spread(staged_sc[0:P:2, W3_AT:W5_AT], w3_scales[0].rearrange("q (n c) -> (q n) c", n=4))
-        for b in range(2):
-            load_spread(staged_sc[0:P:2, W5_AT + P * b:W5_AT + P * (b + 1)], w5_scales[b].rearrange("q (n c) -> (q n) c", n=4))
-        x10 = load_w2(1, 0)
+        load_spread(tab_sc[0:P:4, :], tab_scales)
         list3 = load_list(offs3, "list3")
-        t0 = load_bytes(tab_pass(tab_words, 0), "tab_w0")
+        x0 = load_w2(0)
+        load_spread(tab3_sc[0:P:8, :], tab3_scales)
+        u0 = load_bytes(tab_pass(tab2_words, 0), "tab2_w0")
+        load_spread(planes2[0:P:8, W5_AT:V3_AT].rearrange("p (a c) -> p a c", a=2), w5_scales)
+        load_spread(planes2[0:P:8, W3_AT:SECOND_END], w3_scales)
+        list2 = load_list(offs2, "list2")
+        x1 = load_w2(1)
         u1 = load_bytes(tab_pass(tab2_words, 1), "tab2_w1")
-        t3 = load_bytes(tab3_words[0], "tab3_w")
-        x20 = load_w2(2, 0)
-        u2 = load_bytes(tab_pass(tab2_words, 2), "tab2_w2")
+        t0 = load_bytes(tab_pass(tab_words, 0), "tab_w0")
+        x2 = load_w2(2)
         t1 = load_bytes(tab_pass(tab_words, 1), "tab_w1")
-        x01 = load_w2(0, 1)
+        u2 = load_bytes(tab_pass(tab2_words, 2), "tab2_w2")
+        t3 = load_bytes(tab3_words[0], "tab3_w")
         w3_sb = load_bytes(tab_pass(w3_words, 0), "w3_sb")
-        x11 = load_w2(1, 1)
-        x21 = load_w2(2, 1)
         y0 = load_rows(w4[0:K_PASS, :], "w4_raw0")
-        y1 = [load_rows(w4[K_PASS:2 * K_PASS, 256 * u:256 * (u + 1)], "w4_raw1%d" % u) for u in range(2)]
 
         w1_perm = held([P, 2, 2048], U8, "w1_perm")
         for a in range(2):
             nc.vector.tensor_copy(w1_perm[:, a, :].bitcast(U16).rearrange("p (b t m) -> p b t m", t=PACK, m=P),
                                   w1_raw[:, a, :].bitcast(U16).rearrange("p (b m t) -> p b t m", t=PACK, m=P))
-        nc.vector.tensor_copy(staged_sc[:, 0:W3_AT].rearrange("p (t m) -> p t m", t=PACK),
-                              w1_sc_raw[:].rearrange("p (m t) -> p t m", t=PACK))
+        nc.vector.tensor_copy(planes0[:, W1_AT:V_AT].rearrange("p (b t m) -> p b t m", t=PACK, m=P),
+                              w1_sc_raw[:].rearrange("p (b m t) -> p b t m", t=PACK, m=P))
         v_sc_rows = gather(tab_sc[:], list1, U8, "v_sc_rows")
-        for q in range(4):
-            nc.gpsimd.dma_start(v_planes[32 * q:32 * q + 4, :, :].bitcast(I32), v_sc_rows[32 * q:32 * q + 32:4, :].bitcast(I32))
-        for q in range(4):
-            nc.gpsimd.dma_start(w_planes[32 * q:32 * q + 4, :, :].bitcast(I32), staged_sc[32 * q:32 * q + 32:2, :].bitcast(I32))
-        q00 = quantise_w2(x00, "SS", ["g00"], "w2q00")
-        v2_words[0] = gather(u0[:], list2, U32, "v2_w0")
-        v2_sc = gather(tab2_sc[:], list2, U8, "v2_sc")
-        v3_sc = gather(tab3_sc[:], list3, U8, "v3_sc")
+        nc.vector.tensor_copy(planes0[:, V_AT:FIRST_END].bitcast(I32), v_sc_rows[:].bitcast(I32))
+        for r in range(1, 4):
+            nc.gpsimd.dma_start(planes0[r:P:32, :].bitcast(I32), planes0[8 * r:P:32, :].bitcast(I32))
+        for r in range(4):
+            nc.gpsimd.dma_start(planes[1][r:P:32, :].bitcast(I32), planes0[8 * r + 4:P:32, :].bitcast(I32))
+        v3_sc_rows = gather(tab3_sc[:], list3, U8, "v3_sc_rows")
+        nc.vector.tensor_copy(planes2[:, V3_AT:W3_AT].bitcast(I32), v3_sc_rows[:].bitcast(I32))
+        for r in range(1, 4):
+            nc.sync.dma_start(planes2[r:P:32, :].bitcast(I32), planes2[8 * r:P:32, :].bitcast(I32))
 
         v_words = {}
         w4q = [(held([P, K_PASS], U32, "w4_codes%d" % b), held([P, K_PASS], U8, "w4_scales%d" % b)) for b in range(2)]
@@ -239,45 +246,71 @@ def tile_list_fixture_surplus_scores_kernel(
             cols = slice(256 * u, 256 * (u + 1))
             quantise(grouped[:].rearrange("p c i -> p (c i)"), w4q[b][0][:, cols], w4q[b][1][:, cols])
 
-        bowl_passes(0, 0, q00, True, False)
-        q10 = quantise_w2(x10, "SS", ["g10a", "g10b"], "w2q10")
-        v_words[0] = gather(t0[:], list1, U32, "v_w0", "g10a")
-        v2_words[1] = gather(u1[:], list2, U32, "v2_w1", "g10b")
-        bowl_passes(0, 1, q10, False, False)
-        bat_passes(0, 0, False, False)
-        bat_passes(1, 0, True, False)
-        v3_words = gather(t3[:], list3, U16, "v3_w", "tab2_w1")
-        q20 = quantise_w2(x20, "SS", ["g20"], "w2q20")
-        v2_words[2] = gather(u2[:], list2, U32, "v2_w2", "g20")
-        bowl_passes(0, 2, q20, False, False)
-        v_words[1] = gather(t1[:], list1, U32, "v_w1", "tab2_w2")
-        bat_passes(0, 1, False, True)
-        bat_passes(1, 1, False, False)
-        q01 = quantise_w2(x01, "VV", ["tab_w1"], "w2q01")
-        bowl_passes(1, 0, q01, False, False)
-        h[0] = surplus(0, 2)
+        def w2_half(raw, b):
+            return raw[:, :, b * K_PASS:(b + 1) * K_PASS]
+
+        q00 = quantise_w2(w2_half(x0, 0), "SS", ["g00"], "w2q00")
+        v2_words[0] = gather_whole(u0[:], list2, "v2_w0")
+        v2_sc = gather(tab2_sc[:], list2, U8, "v2_sc")
+        q01 = quantise_w2(w2_half(x0, 1), "SS", ["g01"], "w2q01")
+        for b, w2q in enumerate((q00, q01)):
+            for c in range(CHUNKS):
+                bowl_chunk(b, 0, c, w2q, True)
+        q10 = quantise_w2(w2_half(x1, 0), "SS", ["g10"], "w2q10")
+        v2_words[1] = gather_whole(u1[:], list2, "v2_w1", "g10")
+        w5_sb = load_passes(w5_words, "w5_sb", "tab2_w1")
+        q11 = quantise_w2(w2_half(x1, 1), "SS", ["g11a", "g11b"], "w2q11")
+        y1 = load_rows(w4[K_PASS:2 * K_PASS, :], "w4_raw1", "w2_raw1")
+        v_words[0] = [gather_half(t0[:], list1, 0, "v_w00", "g11a")]
+        for b, w2q in enumerate((q10, q11)):
+            for c in range(CHUNKS):
+                bowl_chunk(b, 1, c, w2q, False)
+        for b in range(2):
+            for c in range(2):
+                bat_chunk(b, 0, c, False)
+        q20 = quantise_w2(w2_half(x2, 0), "VS", ["g11b", "g20"], "w2q20")
+        v_words[0].append(gather_half(t0[:], list1, 1, "v_w01", "g11b"))
+        for b in range(2):
+            for c in range(2, 4):
+                bat_chunk(b, 0, c, False)
+        v_words[1] = gather_whole(t1[:], list1, "v_w1", "g20")
+        q21 = quantise_w2(w2_half(x2, 1), "SS", ["g21"], "w2q21")
+        for c in range(CHUNKS):
+            bat_chunk(0, 1, c, False)
+        v2_words[2] = [gather_half(u2[:], list2, 0, "v2_w20", "g21")]
+        v2_words[2].append(gather_half(u2[:], list2, 1, "v2_w21", "tab_w1"))
+        for c in range(CHUNKS):
+            bowl_chunk(0, 2, c, q20, False, True)
+        for c in range(CHUNKS):
+            bowl_chunk(1, 2, c, q21, False)
+            bat_chunk(1, 1, c, True)
+        v3_words = gather(t3[:], list3, U16, "v3_w", "tab2_w2")
+        d = [[evacuate(b, half) for half in range(2)] for b in range(2)]
         out_banks = [psum.tile([P, S], F32, name="bank%d" % n) for n in range(N_TILES)]
         for n in range(N_TILES):
             ground_pass(n, True, False)
-        q11 = quantise_w2(x11, "SS", ["d00"], "w2q11")
-        w5_sb = load_passes(w5_words, "w5_sb", "w2_raw11")
-        bowl_passes(1, 1, q11, False, False)
-        q21 = quantise_w2(x21, "VS", ["part021", "d02"], "w2q21")
-        bowl_passes(1, 2, q21, False, True)
-        g0 = [w4_half(0, 0, y0[:, :, 0:256], "S", "d00"), w4_half(0, 1, y0[:, :, 256:512], "V", "d02")]
-        quantise_w4_half(0, 1, g0[1])
-        quantise_w4_half(0, 0, g0[0])
-        for n in range(N_TILES):
-            hp_pass(0, n, 0, S, False, False)
-        quantise_w4_half(1, 0, w4_half(1, 0, y1[0][:], "V", "d00"))
+        surplus(0, 0, d[0][0])
+        g0 = [w4_half(0, 0, y0[:, :, 0:256], "V", "part001"), w4_half(0, 1, y0[:, :, 256:512], "S", "d00")]
+        surplus(0, 1, d[0][1])
         for n in range(N_TILES):
             hn_pass(0, n, 0, S)
-        h[1] = surplus(1, 2)
-        quantise_w4_half(1, 1, w4_half(1, 1, y1[1][:], "S", "d10"))
-        for half in range(2):
-            for n in range(N_TILES):
-                for c in range(2):
-                    hn_pass(1, n, (2 * half + c) * CHUNK, CHUNK)
+        surplus(1, 0, d[1][0])
         for n in range(N_TILES):
-            hp_pass(1, n, 0, S, False, True)
+            for c in range(2):
+                hn_pass(1, n, c * CHUNK, CHUNK)
+        for u in range(2):
+            quantise_w4_half(0, u, g0[u])
+        for n in range(N_TILES):
+            hp_pass(0, n, 0, S, False, False)
+        quantise_w4_half(1, 0, w4_half(1, 0, y1[:, :, 0:256], "S", "d01"))
+        for n in range(2):
+            hp_pass(1, n, 0, 2 * CHUNK, False, False)
+        g1b = w4_half(1, 1, y1[:, :, 256:512], "S", "d10")
+        surplus(1, 1, d[1][1], "d01")
+        quantise_w4_half(1, 1, g1b)
+        for n in range(N_TILES):
+            for c in range(2, 4):
+                hn_pass(1, n, c * CHUNK, CHUNK)
+            j0 = 2 * CHUNK if n < 2 else 0
+            hp_pass(1, n, j0, S - j0, False, True)
             finish(n, "SVSV"[n])

@@ -22,6 +22,8 @@ CHUNKS = S // CHUNK
 N_TILES = 4
 FLOPS = 2 * S * (1024 * 1024 + 1536 * 1024 + 2 * 1024 * 512 + 512 * 512)
 
+SLOT = 2048
+
 W1_AT, V_AT, FIRST_END = 0, 1024, 1536
 W5_AT, V3_AT, W3_AT, SECOND_END = 0, 1024, 1536, 2048
 
@@ -34,6 +36,7 @@ def tile_list_fixture_surplus_scores_kernel(
     with ExitStack() as ctx:
         keep = ctx.enter_context(tc.tile_pool(name="keep", bufs=1))
         ring = ctx.enter_context(tc.tile_pool(name="ring", bufs=4))
+        stage = ctx.enter_context(tc.tile_pool(name="stage", bufs=1))
         psum = ctx.enter_context(tc.psum_pool(name="psum", bufs=1))
 
         def held(shape, dtype, name, tag=None):
@@ -44,15 +47,18 @@ def tile_list_fixture_surplus_scores_kernel(
             engine.memset(tile[:].bitcast(I32), 0)
             return tile
 
-        w1_sc_raw = zeroed([P, 1024], "w1_sc_raw", nc.gpsimd)
-        tab_sc = zeroed([P, 2048], "tab_sc", nc.gpsimd)
-        tab2_sc = zeroed([P, 2048], "tab2_sc", nc.vector)
+        def staged(shape, dtype, name, slot):
+            return stage.tile(shape, dtype, name=name, offset=int(slot * SLOT), align_bytes=64)
+
+        tab_sc = zeroed([P, 2048], "tab_sc", nc.vector)
+        w1_sc_raw = zeroed([P, 1024], "w1_sc_raw", nc.vector)
+        tab2_sc = zeroed([P, 2048], "tab2_sc", nc.gpsimd)
         tab3_sc = zeroed([P, 1024], "tab3_sc", nc.vector)
         planes0 = held([P, FIRST_END], U8, "planes0")
-        planes = [planes0, zeroed([P, FIRST_END], "planes1", nc.vector)]
         planes2 = held([P, SECOND_END], U8, "planes2")
         nc.vector.memset(planes2[:, W5_AT:V3_AT].bitcast(I32), 0)
         nc.vector.memset(planes2[:, W3_AT:SECOND_END].bitcast(I32), 0)
+        planes = [planes0, zeroed([P, FIRST_END], "planes1", nc.vector)]
 
         def load_list(src, name):
             tile = keep.tile([P, S // 16], U16, name=name)
@@ -80,23 +86,16 @@ def tile_list_fixture_surplus_scores_kernel(
         def load_w2(a):
             return load_rows(w2[a * K_PASS:(a + 1) * K_PASS, :], "w2_raw%d" % a)
 
-        def gather_into(dst, window, offsets, dtype):
-            nc.vector.tensor_copy(dst.bitcast(dtype), window.bitcast(dtype).indirect(offsets[:]))
+        def gather(dst, window, offsets, dtype):
+            nc.vector.tensor_copy(dst.bitcast(dtype), window.bitcast(dtype).indirect(offsets))
+            return dst
 
-        def gather(window, offsets, dtype, name, tag=None):
-            width = {U32: 4, U16: 2, U8: 1}[dtype]
-            tile = held([P, S * width], U8, name, tag)
-            gather_into(tile[:], window, offsets, dtype)
-            return tile
-
-        def gather_whole(window, offsets, name, tag=None):
-            tile = gather(window, offsets, U32, name, tag)
+        def gather_whole(window, offsets, name, slot):
+            tile = gather(staged([P, 4 * S], U8, name, slot)[:], window[:], offsets[:], U32)
             return [tile[:, 0:2 * S], tile[:, 2 * S:4 * S]]
 
-        def gather_half(window, offsets, half, name, tag=None):
-            tile = held([P, 2 * S], U8, name, tag)
-            nc.vector.tensor_copy(tile[:].bitcast(U32), window.bitcast(U32).indirect(offsets[:, 16 * half:16 * (half + 1)]))
-            return tile[:]
+        def gather_half(window, offsets, half, name, slot):
+            return gather(staged([P, 2 * S], U8, name, slot)[:], window[:], offsets[:, 16 * half:16 * (half + 1)], U32)
 
         def cast(engine, dst, src, factor):
             if engine == "S":
@@ -107,21 +106,25 @@ def tile_list_fixture_surplus_scores_kernel(
         def quantise(grouped, codes, scales):
             nc.vector.quantize_mx(out=codes.bitcast(E4M3), scales=scales, in_=grouped)
 
-        def quantise_w2(raw, engines, tags, name):
-            codes = held([P, K_PASS], U32, name + "_codes")
-            scales = held([P, K_PASS], U8, name + "_scales")
-            if len(tags) == 1:
-                whole = held([P, PACK, P, PACK], BF16, name + "_grouped", tags[0])
-                staged = [whole[:, 0:2, :, :], whole[:, 2:4, :, :]]
-            else:
-                staged = [held([P, 2, P, PACK], BF16, name + "_grouped%d" % h, tags[h])[:] for h in range(2)]
-            for h, engine in enumerate(engines):
-                src = raw.rearrange("p i (m t) -> p m i t", t=PACK)[:, :, :, 2 * h:2 * h + 2]
-                cast(engine, staged[h].rearrange("p t m i -> p m i t"), src, -1.0)
-            for h, grouped in enumerate(staged):
-                cols = slice(2 * h * P, 2 * (h + 1) * P)
-                quantise(grouped.rearrange("p t m i -> p (t m i)"), codes[:, cols], scales[:, cols])
-            return codes, scales
+        w2q = {(a, b): (held([P, K_PASS], U32, "w2_codes%d%d" % (a, b)), held([P, K_PASS], U8, "w2_scales%d%d" % (a, b)))
+               for a in range(3) for b in range(2) if (a, b) != (2, 1)}
+        w2q[2, 1] = (staged([P, K_PASS], U32, "w2_codes21", 25), held([P, K_PASS], U8, "w2_scales21"))
+
+        def round_w2(raw, b, h, engine, dst):
+            src = raw[:, :, b * K_PASS:(b + 1) * K_PASS].rearrange("p i (m t) -> p m i t", t=PACK)[:, :, :, 2 * h:2 * h + 2]
+            cast(engine, dst.rearrange("p t m i -> p m i t"), src, -1.0)
+            return dst
+
+        def quantise_w2(a, b, h, grouped):
+            cols = slice(2 * h * P, 2 * (h + 1) * P)
+            quantise(grouped.rearrange("p t m i -> p (t m i)"), w2q[a, b][0][:, cols], w2q[a, b][1][:, cols])
+
+        def pair(name, slot):
+            whole = staged([P, PACK, P, PACK], BF16, name, slot)
+            return [whole[:, 0:2, :, :], whole[:, 2:4, :, :]]
+
+        def single(name, slot):
+            return staged([P, 2, P, PACK], BF16, name, slot)[:]
 
         def tab_pass(words, a):
             return words[a].rearrange("p t i -> p (t i)")
@@ -132,57 +135,57 @@ def tile_list_fixture_surplus_scores_kernel(
 
         d_banks = [[psum.tile([P, PACK, CHUNK], F32, name="bank%d" % (b * CHUNKS + c)) for c in range(CHUNKS)] for b in range(2)]
 
-        def bowl_chunk(b, a, c, w2q, first, last=False):
-            codes, scales = w2q
+        def bowl_chunk(b, a, c, first=False, last=False):
+            codes, scales = w2q[a, b]
             for t in range(PACK):
                 mx(d_banks[b][c][:, t, :], codes[:, t * P:(t + 1) * P], scales[:, t * P:(t + 1) * P], E4M3,
                    v2_words[a][c // 2][:, 4 * (c % 2) * CHUNK:4 * (c % 2 + 1) * CHUNK], v2_sc[4 * (a + 1):P, c * CHUNK:(c + 1) * CHUNK], E4M3,
                    first and t == 0, last and t == PACK - 1)
 
-        def bat_chunk(b, a, c, last):
+        def bat_chunk(b, a, c, first=False, last=False):
             for t in range(PACK):
                 col = b * K_PASS + t * P
                 mx(d_banks[b][c][:, t, :], w1_perm[:, a, 2 * col:2 * (col + P)],
                    planes[a][:, W1_AT + col:W1_AT + col + P], E2M1,
                    v_words[a][c // 2][:, 4 * (c % 2) * CHUNK:4 * (c % 2 + 1) * CHUNK],
                    planes[a][:, V_AT + c * CHUNK:V_AT + (c + 1) * CHUNK], E4M3,
-                   False, last and t == PACK - 1)
+                   first and t == 0, last and t == PACK - 1)
 
         h = [[(held([P, S], U32, "h_codes%d%d" % (b, s)), held([P, S], U8, "h_scales%d%d" % (b, s))) for s in range(2)]
              for b in range(2)]
 
-        def evacuate(b, half):
-            d = held([P, 2, CHUNK, PACK], BF16, "d%d%d" % (b, half))
+        def evacuate(b, half, slot):
+            d = staged([P, 2, CHUNK, PACK], BF16, "d%d%d" % (b, half), slot)
             for g in range(2):
                 nc.scalar.copy(d[:, g, :, :], d_banks[b][2 * half + g][:].rearrange("p t j -> p j t"))
             return d
 
-        def surplus(b, half, d, tag=None):
-            flat = d[:].rearrange("p g j t -> p (g j t)")
+        def surplus(b, half, d, slot, banks=slice(0, 2)):
+            flat = d[:, banks, :, :].rearrange("p g j t -> p (g j t)")
             parts = []
-            for s, op in enumerate((ALU.max, ALU.min)):
-                part = held([P, 2 * CHUNK * PACK], BF16, "part%d%d%d" % (b, half, s), tag if s == 0 else None)
+            for s, op in ((1, ALU.min), (0, ALU.max)):
+                part = staged([P, flat.shape[1]], BF16, "part%d%d%d%d" % (b, half, banks.start, s), slot + s)
                 nc.vector.tensor_scalar(part[:], flat, 0.0, None, op)
-                parts.append(part)
-            cols = slice(2 * half * CHUNK, 2 * (half + 1) * CHUNK)
-            for s in range(2):
-                quantise(parts[s][:], h[b][s][0][:, cols], h[b][s][1][:, cols])
+                parts.append((s, part))
+            cols = slice((2 * half + banks.start) * CHUNK, (2 * half + banks.stop) * CHUNK)
+            for s, part in parts:
+                quantise(part[:], h[b][s][0][:, cols], h[b][s][1][:, cols])
 
-        def hp_pass(b, n, j0, width, first, last):
+        def hp_pass(b, n, j0, width, last=False):
             codes, scales = w4q[b]
             cols = slice(j0, j0 + width)
             mx(out_banks[n][:, cols], codes[:, n * P:(n + 1) * P], scales[:, n * P:(n + 1) * P], E4M3,
-               h[b][0][0][:, cols], h[b][0][1][:, cols], E4M3, first, last)
+               h[b][0][0][:, cols], h[b][0][1][:, cols], E4M3, False, last)
 
-        def hn_pass(b, n, j0, width):
+        def hn_pass(b, n, j0, width, first=False):
             at = W5_AT + b * K_PASS + n * P
             cols = slice(j0, j0 + width)
             mx(out_banks[n][:, cols], w5_sb[:, b, 2 * n * P:2 * (n + 1) * P], planes2[:, at:at + P], E2M1,
-               h[b][1][0][:, cols], h[b][1][1][:, cols], E4M3, False, False)
+               h[b][1][0][:, cols], h[b][1][1][:, cols], E4M3, first, False)
 
-        def ground_pass(n, first, last):
+        def ground_pass(n):
             mx(out_banks[n][:], w3_sb[:, 4 * n * P:4 * (n + 1) * P], planes2[:, W3_AT + n * P:W3_AT + (n + 1) * P], E4M3,
-               v3_words[:], planes2[:, V3_AT:V3_AT + S], E2M1, first, last)
+               v3_words, planes2[:, V3_AT:V3_AT + S], E2M1, True, False)
 
         def finish(n, engine):
             result = ring.tile([P, S], F32, name="result")
@@ -192,125 +195,150 @@ def tile_list_fixture_surplus_scores_kernel(
                 nc.vector.tensor_copy(result[:], out_banks[n][:])
             nc.sync.dma_start(out[n * P:(n + 1) * P, :], result[:])
 
-        v2_words = {}
+        w4q = [(held([P, K_PASS], U32, "w4_codes%d" % b), held([P, K_PASS], U8, "w4_scales%d" % b)) for b in range(2)]
+
+        def round_w4(b, tiles, raw, engine, slot):
+            cols = slice(tiles.start * P, tiles.stop * P)
+            grouped = staged([P, len(tiles) * P, PACK], BF16, "w4_grouped%d%d" % (b, tiles.start), slot)
+            cast(engine, grouped[:].rearrange("p (c e) i -> p c i e", e=4),
+                 raw[:, :, cols].rearrange("p i (c e) -> p c i e", e=4), 1.0)
+            return b, cols, grouped
+
+        def quantise_w4(piece):
+            b, cols, grouped = piece
+            quantise(grouped[:].rearrange("p c i -> p (c i)"), w4q[b][0][:, cols], w4q[b][1][:, cols])
+
+        v_words, v2_words = {}, {}
 
         for q in range(4):
             nc.gpsimd.dma_start(tab2_sc[32 * q + 4:32 * q + 16, :].bitcast(I32), tab2_scales[:, 4 * q:4 * q + 4, :].bitcast(I32))
         w1_raw = load_passes(w1_words, "w1_raw")
-        load_spread(w1_sc_raw[0:P:4, :], w1_scales)
         list1 = load_list(offs, "list1")
-        load_spread(tab_sc[0:P:4, :], tab_scales)
         list3 = load_list(offs3, "list3")
+        load_spread(tab_sc[0:P:4, :], tab_scales)
+        load_spread(w1_sc_raw[0:P:4, :], w1_scales)
         x0 = load_w2(0)
         load_spread(tab3_sc[0:P:8, :], tab3_scales)
+        list2 = load_list(offs2, "list2")
         u0 = load_bytes(tab_pass(tab2_words, 0), "tab2_w0")
         load_spread(planes2[0:P:8, W5_AT:V3_AT].rearrange("p (a c) -> p a c", a=2), w5_scales)
+        t0 = load_bytes(tab_pass(tab_words, 0), "tab_w0")
         load_spread(planes2[0:P:8, W3_AT:SECOND_END], w3_scales)
-        list2 = load_list(offs2, "list2")
         x1 = load_w2(1)
         u1 = load_bytes(tab_pass(tab2_words, 1), "tab2_w1")
-        t0 = load_bytes(tab_pass(tab_words, 0), "tab_w0")
         x2 = load_w2(2)
         t1 = load_bytes(tab_pass(tab_words, 1), "tab_w1")
         u2 = load_bytes(tab_pass(tab2_words, 2), "tab2_w2")
         t3 = load_bytes(tab3_words[0], "tab3_w")
         w3_sb = load_bytes(tab_pass(w3_words, 0), "w3_sb")
-        y0 = load_rows(w4[0:K_PASS, :], "w4_raw0")
 
-        w1_perm = held([P, 2, 2048], U8, "w1_perm")
-        for a in range(2):
-            nc.vector.tensor_copy(w1_perm[:, a, :].bitcast(U16).rearrange("p (b t m) -> p b t m", t=PACK, m=P),
-                                  w1_raw[:, a, :].bitcast(U16).rearrange("p (b m t) -> p b t m", t=PACK, m=P))
+        v_sc_rows = gather(held([P, S], U8, "v_sc_rows")[:], tab_sc[:], list1[:], U8)
         nc.vector.tensor_copy(planes0[:, W1_AT:V_AT].rearrange("p (b t m) -> p b t m", t=PACK, m=P),
                               w1_sc_raw[:].rearrange("p (b m t) -> p b t m", t=PACK, m=P))
-        v_sc_rows = gather(tab_sc[:], list1, U8, "v_sc_rows")
-        nc.vector.tensor_copy(planes0[:, V_AT:FIRST_END].bitcast(I32), v_sc_rows[:].bitcast(I32))
+        nc.vector.tensor_copy(planes0[:, V_AT:FIRST_END].bitcast(I32), v_sc_rows.bitcast(I32))
         for r in range(1, 4):
             nc.gpsimd.dma_start(planes0[r:P:32, :].bitcast(I32), planes0[8 * r:P:32, :].bitcast(I32))
         for r in range(4):
             nc.gpsimd.dma_start(planes[1][r:P:32, :].bitcast(I32), planes0[8 * r + 4:P:32, :].bitcast(I32))
-        v3_sc_rows = gather(tab3_sc[:], list3, U8, "v3_sc_rows")
-        nc.vector.tensor_copy(planes2[:, V3_AT:W3_AT].bitcast(I32), v3_sc_rows[:].bitcast(I32))
+        w1_perm = held([P, 2, 2048], U8, "w1_perm")
+        for a in range(2):
+            nc.vector.tensor_copy(w1_perm[:, a, :].bitcast(U16).rearrange("p (b t m) -> p b t m", t=PACK, m=P),
+                                  w1_raw[:, a, :].bitcast(U16).rearrange("p (b m t) -> p b t m", t=PACK, m=P))
+        v2_sc = gather(held([P, S], U8, "v2_sc")[:], tab2_sc[:], list2[:], U8)
+        v3_sc_rows = gather(held([P, S], U8, "v3_sc_rows")[:], tab3_sc[:], list3[:], U8)
+        nc.vector.tensor_copy(planes2[:, V3_AT:W3_AT].bitcast(I32), v3_sc_rows.bitcast(I32))
         for r in range(1, 4):
             nc.sync.dma_start(planes2[r:P:32, :].bitcast(I32), planes2[8 * r:P:32, :].bitcast(I32))
 
-        v_words = {}
-        w4q = [(held([P, K_PASS], U32, "w4_codes%d" % b), held([P, K_PASS], U8, "w4_scales%d" % b)) for b in range(2)]
-
-        def w4_half(b, u, raw, engine, tag):
-            grouped = held([P, 256, PACK], BF16, "w4_grouped%d%d" % (b, u), tag)
-            cast(engine, grouped[:].rearrange("p (c e) i -> p c i e", e=4), raw.rearrange("p i (c e) -> p c i e", e=4), 1.0)
-            return grouped
-
-        def quantise_w4_half(b, u, grouped):
-            cols = slice(256 * u, 256 * (u + 1))
-            quantise(grouped[:].rearrange("p c i -> p (c i)"), w4q[b][0][:, cols], w4q[b][1][:, cols])
-
-        def w2_half(raw, b):
-            return raw[:, :, b * K_PASS:(b + 1) * K_PASS]
-
-        q00 = quantise_w2(w2_half(x0, 0), "SS", ["g00"], "w2q00")
-        v2_words[0] = gather_whole(u0[:], list2, "v2_w0")
-        v2_sc = gather(tab2_sc[:], list2, U8, "v2_sc")
-        q01 = quantise_w2(w2_half(x0, 1), "SS", ["g01"], "w2q01")
-        for b, w2q in enumerate((q00, q01)):
+        g = [pair("g00", 0), pair("g01", 2)]
+        for b in range(2):
+            for hh in range(2):
+                round_w2(x0, b, hh, "S", g[b][hh])
+        for hh in range(2):
+            quantise_w2(0, 0, hh, g[0][hh])
+        v2_words[0] = gather_whole(u0, list2, "v2_w0", 0)
+        for hh in range(2):
+            quantise_w2(0, 1, hh, g[1][hh])
+        v_words[0] = [gather_half(t0, list1, 0, "v_w00", 2)]
+        w5_sb = load_passes(w5_words, "w5_sb", "w2_raw0")
+        for b in range(2):
             for c in range(CHUNKS):
-                bowl_chunk(b, 0, c, w2q, True)
-        q10 = quantise_w2(w2_half(x1, 0), "SS", ["g10"], "w2q10")
-        v2_words[1] = gather_whole(u1[:], list2, "v2_w1", "g10")
-        w5_sb = load_passes(w5_words, "w5_sb", "tab2_w1")
-        q11 = quantise_w2(w2_half(x1, 1), "SS", ["g11a", "g11b"], "w2q11")
-        y1 = load_rows(w4[K_PASS:2 * K_PASS, :], "w4_raw1", "w2_raw1")
-        v_words[0] = [gather_half(t0[:], list1, 0, "v_w00", "g11a")]
-        for b, w2q in enumerate((q10, q11)):
-            for c in range(CHUNKS):
-                bowl_chunk(b, 1, c, w2q, False)
+                bowl_chunk(b, 0, c, True)
         for b in range(2):
             for c in range(2):
-                bat_chunk(b, 0, c, False)
-        q20 = quantise_w2(w2_half(x2, 0), "VS", ["g11b", "g20"], "w2q20")
-        v_words[0].append(gather_half(t0[:], list1, 1, "v_w01", "g11b"))
+                bat_chunk(b, 0, c)
+        g = [pair("g10", 4), pair("g11", 6)]
+        for b in range(2):
+            for hh in range(2):
+                round_w2(x1, b, hh, "S", g[b][hh])
+        for hh in range(2):
+            quantise_w2(1, 0, hh, g[0][hh])
+        v2_words[1] = gather_whole(u1, list2, "v2_w1", 4)
+        for hh in range(2):
+            quantise_w2(1, 1, hh, g[1][hh])
+        y0 = load_rows(w4[0:K_PASS, :], "w4_raw0", "tab2_w1")
+        y1 = load_rows(w4[K_PASS:2 * K_PASS, :], "w4_raw1", "w2_raw1")
+        for b in range(2):
+            for c in range(CHUNKS):
+                bowl_chunk(b, 1, c)
+        g20 = [round_w2(x2, 0, 0, "V", single("g200", 6)), round_w2(x2, 0, 1, "S", single("g201", 8))]
+        g21 = pair("g21", 9)
+        for hh in range(2):
+            round_w2(x2, 1, hh, "S", g21[hh])
+        v_words[0].append(gather_half(t0, list1, 1, "v_w01", 7))
         for b in range(2):
             for c in range(2, 4):
-                bat_chunk(b, 0, c, False)
-        v_words[1] = gather_whole(t1[:], list1, "v_w1", "g20")
-        q21 = quantise_w2(w2_half(x2, 1), "SS", ["g21"], "w2q21")
+                bat_chunk(b, 0, c)
+        for hh in range(2):
+            quantise_w2(2, 0, hh, g20[hh])
+        v_words[1] = [gather_half(t1, list1, 0, "v_w10", 8), gather_half(t1, list1, 1, "v_w11", 8.5)]
+        for hh in range(2):
+            quantise_w2(2, 1, hh, g21[hh])
         for c in range(CHUNKS):
-            bat_chunk(0, 1, c, False)
-        v2_words[2] = [gather_half(u2[:], list2, 0, "v2_w20", "g21")]
-        v2_words[2].append(gather_half(u2[:], list2, 1, "v2_w21", "tab_w1"))
+            bat_chunk(0, 1, c)
+        v2_words[2] = [gather_half(u2, list2, 0, "v2_w20", 9), gather_half(u2, list2, 1, "v2_w21", 10)]
         for c in range(CHUNKS):
-            bowl_chunk(0, 2, c, q20, False, True)
+            bowl_chunk(0, 2, c, False, True)
         for c in range(CHUNKS):
-            bowl_chunk(1, 2, c, q21, False)
-            bat_chunk(1, 1, c, True)
-        v3_words = gather(t3[:], list3, U16, "v3_w", "tab2_w2")
-        d = [[evacuate(b, half) for half in range(2)] for b in range(2)]
+            bat_chunk(1, 1, c)
+            bowl_chunk(1, 2, c, False, True)
+        v3_words = gather(held([P, 2 * S], U8, "v3_w", "tab2_w2")[:], t3[:], list3[:], U16)
+        d = [[evacuate(b, half, 11 + 2 * b + half) for half in range(2)] for b in range(2)]
         out_banks = [psum.tile([P, S], F32, name="bank%d" % n) for n in range(N_TILES)]
         for n in range(N_TILES):
-            ground_pass(n, True, False)
-        surplus(0, 0, d[0][0])
-        g0 = [w4_half(0, 0, y0[:, :, 0:256], "V", "part001"), w4_half(0, 1, y0[:, :, 256:512], "S", "d00")]
-        surplus(0, 1, d[0][1])
+            ground_pass(n)
+        surplus(0, 0, d[0][0], 23, slice(0, 1))
+        surplus(0, 0, d[0][0], 15, slice(1, 2))
+        surplus(0, 1, d[0][1], 17)
         for n in range(N_TILES):
             hn_pass(0, n, 0, S)
-        surplus(1, 0, d[1][0])
+        surplus(1, 0, d[1][0], 19)
+        a01 = round_w4(0, range(0, 2), y0, "S", 10)
+        b1 = round_w4(1, range(1, 2), y1, "S", 25)
+        b2 = round_w4(1, range(2, 3), y1, "S", 25.5)
+        b3 = round_w4(1, range(3, 4), y1, "S", 14)
         for n in range(N_TILES):
             for c in range(2):
                 hn_pass(1, n, c * CHUNK, CHUNK)
-        for u in range(2):
-            quantise_w4_half(0, u, g0[u])
-        for n in range(N_TILES):
-            hp_pass(0, n, 0, S, False, False)
-        quantise_w4_half(1, 0, w4_half(1, 0, y1[:, :, 0:256], "S", "d01"))
-        for n in range(2):
-            hp_pass(1, n, 0, 2 * CHUNK, False, False)
-        g1b = w4_half(1, 1, y1[:, :, 256:512], "S", "d10")
-        surplus(1, 1, d[1][1], "d01")
-        quantise_w4_half(1, 1, g1b)
+        surplus(1, 1, d[1][1], 21)
         for n in range(N_TILES):
             for c in range(2, 4):
                 hn_pass(1, n, c * CHUNK, CHUNK)
-            j0 = 2 * CHUNK if n < 2 else 0
-            hp_pass(1, n, j0, S - j0, False, True)
-            finish(n, "SVSV"[n])
+        b0 = round_w4(1, range(0, 1), y1, "V", 21)
+        quantise_w4(a01)
+        quantise_w4(b0)
+        quantise_w4(b1)
+        for n in range(2):
+            hp_pass(0, n, 0, S)
+            hp_pass(1, n, 0, S, True)
+        a2 = round_w4(0, range(2, 3), y0, "V", 21)
+        quantise_w4(b2)
+        a3 = round_w4(0, range(3, 4), y0, "V", 25)
+        quantise_w4(a2)
+        quantise_w4(b3)
+        quantise_w4(a3)
+        for n in range(2, 4):
+            hp_pass(1, n, 0, S)
+            hp_pass(0, n, 0, S, True)
+        for n in range(N_TILES):
+            finish(n, "SSVS"[n])

@@ -35,7 +35,6 @@ def tile_list_fixture_surplus_scores_kernel(
     nc = tc.nc
     with ExitStack() as ctx:
         keep = ctx.enter_context(tc.tile_pool(name="keep", bufs=1))
-        ring = ctx.enter_context(tc.tile_pool(name="ring", bufs=4))
         stage = ctx.enter_context(tc.tile_pool(name="stage", bufs=1))
         psum = ctx.enter_context(tc.psum_pool(name="psum", bufs=1))
 
@@ -110,9 +109,9 @@ def tile_list_fixture_surplus_scores_kernel(
                for a in range(3) for b in range(2) if (a, b) != (2, 1)}
         w2q[2, 1] = (staged([P, K_PASS], U32, "w2_codes21", 25), held([P, K_PASS], U8, "w2_scales21"))
 
-        def round_w2(raw, b, h, engine, dst):
-            src = raw[:, :, b * K_PASS:(b + 1) * K_PASS].rearrange("p i (m t) -> p m i t", t=PACK)[:, :, :, 2 * h:2 * h + 2]
-            cast(engine, dst.rearrange("p t m i -> p m i t"), src, -1.0)
+        def round_w2(raw, b, h, engine, dst, rows=slice(0, P)):
+            src = raw[:, :, b * K_PASS:(b + 1) * K_PASS].rearrange("p i (m t) -> p m i t", t=PACK)[:, rows, :, 2 * h:2 * h + 2]
+            cast(engine, dst.rearrange("p t m i -> p m i t")[:, rows, :, :], src, -1.0)
             return dst
 
         def quantise_w2(a, b, h, grouped):
@@ -160,53 +159,74 @@ def tile_list_fixture_surplus_scores_kernel(
                 nc.scalar.copy(d[:, g, :, :], d_banks[b][2 * half + g][:].rearrange("p t j -> p j t"))
             return d
 
-        def surplus(b, half, d, slot, banks=slice(0, 2)):
+        def cut(b, half, d, slot, banks=slice(0, 2)):
             flat = d[:, banks, :, :].rearrange("p g j t -> p (g j t)")
+            cols = slice((2 * half + banks.start) * CHUNK, (2 * half + banks.stop) * CHUNK)
             parts = []
             for s, op in ((1, ALU.min), (0, ALU.max)):
                 part = staged([P, flat.shape[1]], BF16, "part%d%d%d%d" % (b, half, banks.start, s), slot + s)
                 nc.vector.tensor_scalar(part[:], flat, 0.0, None, op)
-                parts.append((s, part))
-            cols = slice((2 * half + banks.start) * CHUNK, (2 * half + banks.stop) * CHUNK)
-            for s, part in parts:
-                quantise(part[:], h[b][s][0][:, cols], h[b][s][1][:, cols])
+                parts.append((part[:], h[b][s][0][:, cols], h[b][s][1][:, cols]))
+            return parts
 
-        def hp_pass(b, n, j0, width, last=False):
-            codes, scales = w4q[b]
-            cols = slice(j0, j0 + width)
-            mx(out_banks[n][:, cols], codes[:, n * P:(n + 1) * P], scales[:, n * P:(n + 1) * P], E4M3,
-               h[b][0][0][:, cols], h[b][0][1][:, cols], E4M3, False, last)
+        def surplus(b, half, d, slot, banks=slice(0, 2)):
+            for part in cut(b, half, d, slot, banks):
+                quantise(*part)
 
-        def hn_pass(b, n, j0, width, first=False):
+        opened = set()
+
+        def out_passes(n, j0, j1, wide, last, run):
+            for lo, hi, bank in out_banks[n]:
+                a, z = max(lo, j0), min(hi, j1)
+                step = z - a if z - a in wide else CHUNK
+                for j in range(a, z, max(step, 1)):
+                    run(bank[:, j - lo:j - lo + step], slice(j, j + step), (n, lo) not in opened, last and j + step == z)
+                    opened.add((n, lo))
+
+        def hp_pass(b, n, j0, j1, last=False):
+            codes, scales = w4q[b, n]
+            out_passes(n, j0, j1, (256, 512), last, lambda dst, cols, start, stop: mx(
+                dst, codes, scales, E4M3,
+                h[b][0][0][:, cols], h[b][0][1][:, cols], E4M3, start, stop))
+
+        def hn_pass(b, n, j0, j1):
             at = W5_AT + b * K_PASS + n * P
-            cols = slice(j0, j0 + width)
-            mx(out_banks[n][:, cols], w5_sb[:, b, 2 * n * P:2 * (n + 1) * P], planes2[:, at:at + P], E2M1,
-               h[b][1][0][:, cols], h[b][1][1][:, cols], E4M3, first, False)
+            out_passes(n, j0, j1, (512,), False, lambda dst, cols, start, stop: mx(
+                dst, w5_sb[:, b, 2 * n * P:2 * (n + 1) * P], planes2[:, at:at + P], E2M1,
+                h[b][1][0][:, cols], h[b][1][1][:, cols], E4M3, start, stop))
 
-        def ground_pass(n):
-            mx(out_banks[n][:], w3_sb[:, 4 * n * P:4 * (n + 1) * P], planes2[:, W3_AT + n * P:W3_AT + (n + 1) * P], E4M3,
-               v3_words, planes2[:, V3_AT:V3_AT + S], E2M1, True, False)
+        def ground_pass(n, j0=0, j1=S):
+            out_passes(n, j0, j1, (512,), False, lambda dst, cols, start, stop: mx(
+                dst, w3_sb[:, 4 * n * P:4 * (n + 1) * P], planes2[:, W3_AT + n * P:W3_AT + (n + 1) * P], E4M3,
+                v3_words[:, 2 * cols.start:2 * cols.stop], planes2[:, V3_AT + cols.start:V3_AT + cols.stop], E2M1, start, stop))
 
-        def finish(n, engine):
-            result = ring.tile([P, S], F32, name="result")
+        def finish(n, piece, engine):
+            lo, hi, bank = out_banks[n][piece]
+            result = held([P, hi - lo], F32, "result%d%d" % (n, piece))
             if engine == "S":
-                nc.scalar.copy(result[:], out_banks[n][:])
+                nc.scalar.copy(result[:], bank[:, 0:hi - lo])
             else:
-                nc.vector.tensor_copy(result[:], out_banks[n][:])
-            nc.sync.dma_start(out[n * P:(n + 1) * P, :], result[:])
+                nc.vector.tensor_copy(result[:], bank[:, 0:hi - lo])
+            nc.sync.dma_start(out[n * P:(n + 1) * P, lo:hi], result[:])
 
-        w4q = [(held([P, K_PASS], U32, "w4_codes%d" % b), held([P, K_PASS], U8, "w4_scales%d" % b)) for b in range(2)]
+        w4q = {}
 
         def round_w4(b, tiles, raw, engine, slot):
             cols = slice(tiles.start * P, tiles.stop * P)
             grouped = staged([P, len(tiles) * P, PACK], BF16, "w4_grouped%d%d" % (b, tiles.start), slot)
             cast(engine, grouped[:].rearrange("p (c e) i -> p c i e", e=4),
                  raw[:, :, cols].rearrange("p i (c e) -> p c i e", e=4), 1.0)
-            return b, cols, grouped
+            return b, tiles, grouped
 
-        def quantise_w4(piece):
-            b, cols, grouped = piece
-            quantise(grouped[:].rearrange("p c i -> p (c i)"), w4q[b][0][:, cols], w4q[b][1][:, cols])
+        def quantise_w4(piece, slot=None):
+            b, tiles, grouped = piece
+            name = "w4_codes%d%d" % (b, tiles.start)
+            shape = [P, len(tiles) * P]
+            codes = held(shape, U32, name) if slot is None else staged(shape, U32, name, slot)
+            scales = held(shape, U8, "w4_scales%d%d" % (b, tiles.start))
+            quantise(grouped[:].rearrange("p c i -> p (c i)"), codes[:], scales[:])
+            for k, n in enumerate(tiles):
+                w4q[b, n] = (codes[:, k * P:(k + 1) * P], scales[:, k * P:(k + 1) * P])
 
         v_words, v2_words = {}, {}
 
@@ -304,12 +324,17 @@ def tile_list_fixture_surplus_scores_kernel(
             bowl_chunk(1, 2, c, False, True)
         v3_words = gather(held([P, 2 * S], U8, "v3_w", "tab2_w2")[:], t3[:], list3[:], U16)
         d = [[evacuate(b, half, 11 + 2 * b + half) for half in range(2)] for b in range(2)]
-        out_banks = [psum.tile([P, S], F32, name="bank%d" % n) for n in range(N_TILES)]
+        def bank(k):
+            return psum.tile([P, S], F32, name="bank%d" % k)
+
+        out_banks = [[(0, 256, bank(0)), (256, S, bank(4))], [(0, S, bank(1))], [(0, S, bank(2))], [(0, 256, bank(3)), (256, S, bank(5))]]
         for n in range(N_TILES):
-            ground_pass(n)
+            ground_pass(n, 0, S if n in (1, 2) else 256)
         surplus(0, 0, d[0][0], 23, slice(0, 1))
         surplus(0, 0, d[0][0], 15, slice(1, 2))
         surplus(0, 1, d[0][1], 17)
+        for n in (0, 3):
+            ground_pass(n, 256, S)
         for n in range(N_TILES):
             hn_pass(0, n, 0, S)
         surplus(1, 0, d[1][0], 19)
@@ -318,27 +343,25 @@ def tile_list_fixture_surplus_scores_kernel(
         b2 = round_w4(1, range(2, 3), y1, "S", 25.5)
         b3 = round_w4(1, range(3, 4), y1, "S", 14)
         for n in range(N_TILES):
-            for c in range(2):
-                hn_pass(1, n, c * CHUNK, CHUNK)
+            hn_pass(1, n, 0, 256)
         surplus(1, 1, d[1][1], 21)
+        b0 = round_w4(1, range(0, 1), y1, "V", 22)
         for n in range(N_TILES):
-            for c in range(2, 4):
-                hn_pass(1, n, c * CHUNK, CHUNK)
-        b0 = round_w4(1, range(0, 1), y1, "V", 21)
-        quantise_w4(a01)
+            hn_pass(1, n, 256, S)
+        quantise_w4(a01, 21)
         quantise_w4(b0)
-        quantise_w4(b1)
+        quantise_w4(b1, 10)
         for n in range(2):
             hp_pass(0, n, 0, S)
             hp_pass(1, n, 0, S, True)
-        a2 = round_w4(0, range(2, 3), y0, "V", 21)
-        quantise_w4(b2)
-        a3 = round_w4(0, range(3, 4), y0, "V", 25)
+        a2 = round_w4(0, range(2, 3), y0, "V", 22)
+        quantise_w4(b2, 25)
         quantise_w4(a2)
-        quantise_w4(b3)
+        a3 = round_w4(0, range(3, 4), y0, "V", 25.5)
+        quantise_w4(b3, 22)
         quantise_w4(a3)
         for n in range(2, 4):
             hp_pass(1, n, 0, S)
             hp_pass(0, n, 0, S, True)
-        for n in range(N_TILES):
-            finish(n, "SSVS"[n])
+        for n, piece, engine in ((0, 0, "S"), (0, 1, "S"), (1, 0, "S"), (2, 0, "S"), (3, 0, "V"), (3, 1, "S")):
+            finish(n, piece, engine)

@@ -17,8 +17,7 @@ P = 128
 PACK = 4
 K_PASS = P * PACK
 S = 512
-CHUNK = 128
-CHUNKS = S // CHUNK
+HALF = S // 2
 N_TILES = 4
 FLOPS = 2 * S * (1024 * 1024 + 1536 * 1024 + 2 * 1024 * 512 + 512 * 512)
 
@@ -53,19 +52,20 @@ def tile_list_fixture_surplus_scores_kernel(
         w1_sc_raw = zeroed([P, 1024], "w1_sc_raw", nc.vector)
         tab2_sc = zeroed([P, 2048], "tab2_sc", nc.gpsimd)
         tab3_sc = zeroed([P, 1024], "tab3_sc", nc.vector)
-        planes0 = held([P, FIRST_END], U8, "planes0")
         planes2 = held([P, SECOND_END], U8, "planes2")
         nc.vector.memset(planes2[:, W5_AT:V3_AT].bitcast(I32), 0)
         nc.vector.memset(planes2[:, W3_AT:SECOND_END].bitcast(I32), 0)
-        planes = [planes0, zeroed([P, FIRST_END], "planes1", nc.vector)]
+        planes1 = zeroed([P, 2 * FIRST_END], "planes1", nc.vector)
+        rows1 = held([P, FIRST_END], U8, "rows1")
 
         def load_list(src, name):
             tile = keep.tile([P, S // 16], U16, name=name)
             nc.sync.dma_start(tile[:], src)
             return tile
 
-        def load_bytes(src, name, tag=None):
-            tile = held([P, src.shape[1]], U8, name, tag)
+        def load_bytes(src, name, tag=None, slot=None):
+            shape = [P, src.shape[1]]
+            tile = held(shape, U8, name, tag) if slot is None else staged(shape, U8, name, slot)
             nc.sync.dma_start(tile[:].bitcast(I32), src.bitcast(I32))
             return tile
 
@@ -82,19 +82,22 @@ def tile_list_fixture_surplus_scores_kernel(
             nc.sync.dma_start(tile[:], src.rearrange("(p i) c -> p i c", i=PACK))
             return tile
 
-        def load_w2(a):
-            return load_rows(w2[a * K_PASS:(a + 1) * K_PASS, :], "w2_raw%d" % a)
+        def load_w2(a, tag=None):
+            return load_rows(w2[a * K_PASS:(a + 1) * K_PASS, :], "w2_raw%d" % a, tag)
+
+        def tab_pass(words, a):
+            return words[a].rearrange("p t i -> p (t i)")
 
         def gather(dst, window, offsets, dtype):
             nc.vector.tensor_copy(dst.bitcast(dtype), window.bitcast(dtype).indirect(offsets))
             return dst
 
-        def gather_whole(window, offsets, name, slot):
-            tile = gather(staged([P, 4 * S], U8, name, slot)[:], window[:], offsets[:], U32)
+        def gather_whole(window, offsets, tile):
+            gather(tile[:], window[:], offsets[:], U32)
             return [tile[:, 0:2 * S], tile[:, 2 * S:4 * S]]
 
-        def gather_half(window, offsets, half, name, slot):
-            return gather(staged([P, 2 * S], U8, name, slot)[:], window[:], offsets[:, 16 * half:16 * (half + 1)], U32)
+        def gather_half(window, offsets, half, tile):
+            return gather(tile[:], window[:], offsets[:, 16 * half:16 * (half + 1)], U32)
 
         def cast(engine, dst, src, factor):
             if engine == "S":
@@ -106,97 +109,82 @@ def tile_list_fixture_surplus_scores_kernel(
             nc.vector.quantize_mx(out=codes.bitcast(E4M3), scales=scales, in_=grouped)
 
         w2q = {(a, b): (held([P, K_PASS], U32, "w2_codes%d%d" % (a, b)), held([P, K_PASS], U8, "w2_scales%d%d" % (a, b)))
-               for a in range(3) for b in range(2) if (a, b) != (2, 1)}
-        w2q[2, 1] = (staged([P, K_PASS], U32, "w2_codes21", 25), held([P, K_PASS], U8, "w2_scales21"))
+               for a in range(3) for b in range(2)}
 
-        def round_w2(raw, b, h, engine, dst, rows=slice(0, P)):
-            src = raw[:, :, b * K_PASS:(b + 1) * K_PASS].rearrange("p i (m t) -> p m i t", t=PACK)[:, rows, :, 2 * h:2 * h + 2]
-            cast(engine, dst.rearrange("p t m i -> p m i t")[:, rows, :, :], src, -1.0)
-            return dst
+        def round_w2(raw, a, b, u, engine, slot, dst=None):
+            if dst is None:
+                dst = staged([P, 2, P, PACK], BF16, "w2_grouped%d%d%d" % (a, b, u), slot)[:]
+            src = raw[:, :, b * K_PASS:(b + 1) * K_PASS].rearrange("p i (m t) -> p m i t", t=PACK)[:, :, :, 2 * u:2 * u + 2]
+            cast(engine, dst.rearrange("p t m i -> p m i t"), src, -1.0)
+            return a, b, u, dst
 
-        def quantise_w2(a, b, h, grouped):
-            cols = slice(2 * h * P, 2 * (h + 1) * P)
+        def quantise_w2(piece):
+            a, b, u, grouped = piece
+            cols = slice(2 * u * P, 2 * (u + 1) * P)
             quantise(grouped.rearrange("p t m i -> p (t m i)"), w2q[a, b][0][:, cols], w2q[a, b][1][:, cols])
-
-        def pair(name, slot):
-            whole = staged([P, PACK, P, PACK], BF16, name, slot)
-            return [whole[:, 0:2, :, :], whole[:, 2:4, :, :]]
-
-        def single(name, slot):
-            return staged([P, 2, P, PACK], BF16, name, slot)[:]
-
-        def tab_pass(words, a):
-            return words[a].rearrange("p t i -> p (t i)")
 
         def mx(dst, lhsT, lhsT_scale, lhsT_fmt, rhs, rhs_scale, rhs_fmt, start, stop):
             nc.tensor.matmul_mx(out=dst, lhsT=lhsT.bitcast(lhsT_fmt), lhsT_scale=lhsT_scale,
                                 rhs=rhs.bitcast(rhs_fmt), rhs_scale=rhs_scale, start=start, stop=stop)
 
-        d_banks = [[psum.tile([P, PACK, CHUNK], F32, name="bank%d" % (b * CHUNKS + c)) for c in range(CHUNKS)] for b in range(2)]
+        d_banks = {(g, b, u): psum.tile([P, 2, HALF], F32, name="bank%d" % (4 * g + 2 * b + u))
+                   for g in range(2) for b in range(2) for u in range(2)}
 
-        def bowl_chunk(b, a, c, first=False, last=False):
+        def bowl(a, g, b, u, first=False, last=False):
             codes, scales = w2q[a, b]
-            for t in range(PACK):
-                mx(d_banks[b][c][:, t, :], codes[:, t * P:(t + 1) * P], scales[:, t * P:(t + 1) * P], E4M3,
-                   v2_words[a][c // 2][:, 4 * (c % 2) * CHUNK:4 * (c % 2 + 1) * CHUNK], v2_sc[4 * (a + 1):P, c * CHUNK:(c + 1) * CHUNK], E4M3,
-                   first and t == 0, last and t == PACK - 1)
+            for e in range(2):
+                cols = slice((2 * u + e) * P, (2 * u + e + 1) * P)
+                mx(d_banks[g, b, u][:, e, :], codes[:, cols], scales[:, cols], E4M3,
+                   v2_words[a][g], v2_sc[4 * (a + 1):P, g * HALF:(g + 1) * HALF], E4M3, first and e == 0, last and e == 1)
 
-        def bat_chunk(b, a, c, first=False, last=False):
-            for t in range(PACK):
-                col = b * K_PASS + t * P
-                mx(d_banks[b][c][:, t, :], w1_perm[:, a, 2 * col:2 * (col + P)],
-                   planes[a][:, W1_AT + col:W1_AT + col + P], E2M1,
-                   v_words[a][c // 2][:, 4 * (c % 2) * CHUNK:4 * (c % 2 + 1) * CHUNK],
-                   planes[a][:, V_AT + c * CHUNK:V_AT + (c + 1) * CHUNK], E4M3,
-                   first and t == 0, last and t == PACK - 1)
+        def bat(a, g, b, u):
+            for e in range(2):
+                col = b * K_PASS + (2 * u + e) * P
+                at = a * FIRST_END
+                mx(d_banks[g, b, u][:, e, :], w1_perm[:, a, 2 * col:2 * (col + P)], planes1[:, at + W1_AT + col:at + W1_AT + col + P], E2M1,
+                   v_words[a][g], planes1[:, at + V_AT + g * HALF:at + V_AT + (g + 1) * HALF], E4M3, False, False)
 
-        h = [[(held([P, S], U32, "h_codes%d%d" % (b, s)), held([P, S], U8, "h_scales%d%d" % (b, s))) for s in range(2)]
-             for b in range(2)]
+        h = {(b, s): (held([P, S], U32, "h_codes%d%d" % (b, s)), held([P, S], U8, "h_scales%d%d" % (b, s)))
+             for b in range(2) for s in range(2)}
 
-        def evacuate(b, half, slot):
-            d = staged([P, 2, CHUNK, PACK], BF16, "d%d%d" % (b, half), slot)
-            for g in range(2):
-                nc.scalar.copy(d[:, g, :, :], d_banks[b][2 * half + g][:].rearrange("p t j -> p j t"))
+        def evacuate(g, b, slot):
+            d = staged([P, 2, HALF, 2], BF16, "d%d%d" % (g, b), slot)
+            for u in range(2):
+                nc.scalar.copy(d[:, u, :, :], d_banks[g, b, u][:].rearrange("p e j -> p j e"))
             return d
 
-        def cut(b, half, d, slot, banks=slice(0, 2)):
-            flat = d[:, banks, :, :].rearrange("p g j t -> p (g j t)")
-            cols = slice((2 * half + banks.start) * CHUNK, (2 * half + banks.stop) * CHUNK)
+        def surplus(g, b, d, slot):
+            cols = slice(g * HALF, (g + 1) * HALF)
             parts = []
             for s, op in ((1, ALU.min), (0, ALU.max)):
-                part = staged([P, flat.shape[1]], BF16, "part%d%d%d%d" % (b, half, banks.start, s), slot + s)
-                nc.vector.tensor_scalar(part[:], flat, 0.0, None, op)
-                parts.append((part[:], h[b][s][0][:, cols], h[b][s][1][:, cols]))
-            return parts
-
-        def surplus(b, half, d, slot, banks=slice(0, 2)):
-            for part in cut(b, half, d, slot, banks):
+                part = staged([P, HALF, 2, 2], BF16, "part%d%d%d" % (g, b, s), slot + s)
+                nc.vector.tensor_scalar(part[:], d[:].rearrange("p u j e -> p j u e"), 0.0, None, op)
+                parts.append((part[:].rearrange("p j u e -> p (j u e)"), h[b, s][0][:, cols], h[b, s][1][:, cols]))
+            for part in parts:
                 quantise(*part)
 
         opened = set()
 
-        def out_passes(n, j0, j1, wide, last, run):
+        def out_passes(n, j0, j1, last, run):
             for lo, hi, bank in out_banks[n]:
                 a, z = max(lo, j0), min(hi, j1)
-                step = z - a if z - a in wide else CHUNK
-                for j in range(a, z, max(step, 1)):
-                    run(bank[:, j - lo:j - lo + step], slice(j, j + step), (n, lo) not in opened, last and j + step == z)
+                if a < z:
+                    run(bank[:, a - lo:z - lo], slice(a, z), (n, lo) not in opened, last)
                     opened.add((n, lo))
 
-        def hp_pass(b, n, j0, j1, last=False):
+        def hp_pass(b, n, last=False):
             codes, scales = w4q[b, n]
-            out_passes(n, j0, j1, (256, 512), last, lambda dst, cols, start, stop: mx(
-                dst, codes, scales, E4M3,
-                h[b][0][0][:, cols], h[b][0][1][:, cols], E4M3, start, stop))
+            out_passes(n, 0, S, last, lambda dst, cols, start, stop: mx(
+                dst, codes, scales, E4M3, h[b, 0][0][:, cols], h[b, 0][1][:, cols], E4M3, start, stop))
 
-        def hn_pass(b, n, j0, j1):
+        def hn_pass(b, n, g):
             at = W5_AT + b * K_PASS + n * P
-            out_passes(n, j0, j1, (512,), False, lambda dst, cols, start, stop: mx(
+            out_passes(n, g * HALF, (g + 1) * HALF, False, lambda dst, cols, start, stop: mx(
                 dst, w5_sb[:, b, 2 * n * P:2 * (n + 1) * P], planes2[:, at:at + P], E2M1,
-                h[b][1][0][:, cols], h[b][1][1][:, cols], E4M3, start, stop))
+                h[b, 1][0][:, cols], h[b, 1][1][:, cols], E4M3, start, stop))
 
-        def ground_pass(n, j0=0, j1=S):
-            out_passes(n, j0, j1, (512,), False, lambda dst, cols, start, stop: mx(
+        def ground_pass(n, j0, j1):
+            out_passes(n, j0, j1, False, lambda dst, cols, start, stop: mx(
                 dst, w3_sb[:, 4 * n * P:4 * (n + 1) * P], planes2[:, W3_AT + n * P:W3_AT + (n + 1) * P], E4M3,
                 v3_words[:, 2 * cols.start:2 * cols.stop], planes2[:, V3_AT + cols.start:V3_AT + cols.stop], E2M1, start, stop))
 
@@ -229,139 +217,127 @@ def tile_list_fixture_surplus_scores_kernel(
                 w4q[b, n] = (codes[:, k * P:(k + 1) * P], scales[:, k * P:(k + 1) * P])
 
         v_words, v2_words = {}, {}
+        pairs = [(b, u) for b in range(2) for u in range(2)]
 
         for q in range(4):
             nc.gpsimd.dma_start(tab2_sc[32 * q + 4:32 * q + 16, :].bitcast(I32), tab2_scales[:, 4 * q:4 * q + 4, :].bitcast(I32))
         w1_raw = load_passes(w1_words, "w1_raw")
         list1 = load_list(offs, "list1")
-        list3 = load_list(offs3, "list3")
         load_spread(tab_sc[0:P:4, :], tab_scales)
         load_spread(w1_sc_raw[0:P:4, :], w1_scales)
         x0 = load_w2(0)
-        load_spread(tab3_sc[0:P:8, :], tab3_scales)
         list2 = load_list(offs2, "list2")
+        list3 = load_list(offs3, "list3")
+        load_spread(tab3_sc[0:P:8, :], tab3_scales)
         u0 = load_bytes(tab_pass(tab2_words, 0), "tab2_w0")
         load_spread(planes2[0:P:8, W5_AT:V3_AT].rearrange("p (a c) -> p a c", a=2), w5_scales)
-        t0 = load_bytes(tab_pass(tab_words, 0), "tab_w0")
         load_spread(planes2[0:P:8, W3_AT:SECOND_END], w3_scales)
-        x1 = load_w2(1)
-        u1 = load_bytes(tab_pass(tab2_words, 1), "tab2_w1")
-        x2 = load_w2(2)
-        t1 = load_bytes(tab_pass(tab_words, 1), "tab_w1")
-        u2 = load_bytes(tab_pass(tab2_words, 2), "tab2_w2")
-        t3 = load_bytes(tab3_words[0], "tab3_w")
-        w3_sb = load_bytes(tab_pass(w3_words, 0), "w3_sb")
+        t0 = load_bytes(tab_pass(tab_words, 0), "tab_w0")
 
         v_sc_rows = gather(held([P, S], U8, "v_sc_rows")[:], tab_sc[:], list1[:], U8)
-        nc.vector.tensor_copy(planes0[:, W1_AT:V_AT].rearrange("p (b t m) -> p b t m", t=PACK, m=P),
+        nc.vector.tensor_copy(rows1[:, W1_AT:V_AT].rearrange("p (b t m) -> p b t m", t=PACK, m=P),
                               w1_sc_raw[:].rearrange("p (b m t) -> p b t m", t=PACK, m=P))
-        nc.vector.tensor_copy(planes0[:, V_AT:FIRST_END].bitcast(I32), v_sc_rows.bitcast(I32))
-        for r in range(1, 4):
-            nc.gpsimd.dma_start(planes0[r:P:32, :].bitcast(I32), planes0[8 * r:P:32, :].bitcast(I32))
-        for r in range(4):
-            nc.gpsimd.dma_start(planes[1][r:P:32, :].bitcast(I32), planes0[8 * r + 4:P:32, :].bitcast(I32))
+        nc.vector.tensor_copy(rows1[:, V_AT:FIRST_END].bitcast(I32), v_sc_rows.bitcast(I32))
+        for q in range(4):
+            nc.gpsimd.dma_start(planes1[32 * q:32 * q + 4, :].rearrange("p (a c) -> p a c", a=2).bitcast(I32),
+                                rows1[32 * q:32 * q + 32:4, :].bitcast(I32))
         w1_perm = held([P, 2, 2048], U8, "w1_perm")
         for a in range(2):
             nc.vector.tensor_copy(w1_perm[:, a, :].bitcast(U16).rearrange("p (b t m) -> p b t m", t=PACK, m=P),
                                   w1_raw[:, a, :].bitcast(U16).rearrange("p (b m t) -> p b t m", t=PACK, m=P))
-        v2_sc = gather(held([P, S], U8, "v2_sc")[:], tab2_sc[:], list2[:], U8)
-        v3_sc_rows = gather(held([P, S], U8, "v3_sc_rows")[:], tab3_sc[:], list3[:], U8)
+        x1 = load_w2(1, "w1_raw")
+        u1 = load_bytes(tab_pass(tab2_words, 1), "tab2_w1")
+
+        g0 = [round_w2(x0, 0, b, u, "S", 20 if (b, u) == (1, 1) else 2 * b + u) for b, u in pairs]
+        x2 = load_w2(2, "w2_raw0")
+        for piece in g0[:2]:
+            quantise_w2(piece)
+        v2_words[0] = gather_whole(u0, list2, held([P, 4 * S], U8, "v2_w0"))
+        for piece in g0[2:]:
+            quantise_w2(piece)
+        v2_sc = gather(staged([P, S], U8, "v2_sc", 20)[:], tab2_sc[:], list2[:], U8)
+        t1 = load_bytes(tab_pass(tab_words, 1), "tab_w1", "tab2_sc")
+        v_words[0] = [gather_half(t0, list1, 0, held([P, 2 * S], U8, "v_w00"))]
+        for b, u in pairs:
+            for g in range(2):
+                bowl(0, g, b, u, True)
+        for b, u in pairs:
+            bat(0, 0, b, u)
+        g1 = [round_w2(x1, 1, b, u, "S", 21 if (b, u) == (0, 0) else 4 + 2 * b + u) for b, u in pairs]
+        for piece in g1[:2]:
+            quantise_w2(piece)
+        u2 = load_bytes(tab_pass(tab2_words, 2), "tab2_w2", slot=21)
+        t3 = load_bytes(tab3_words[0], "tab3_w", slot=5)
+        v2_words[1] = gather_whole(u1, list2, held([P, 4 * S], U8, "v2_w1"))
+        w3_sb = load_bytes(tab_pass(w3_words, 0), "w3_sb", "tab2_w1")
+        for piece in g1[2:]:
+            quantise_w2(piece)
+        v3_sc_rows = gather(staged([P, S], U8, "v3_sc_rows", 7)[:], tab3_sc[:], list3[:], U8)
+        v_words[0].append(gather_half(t0, list1, 1, staged([P, 2 * S], U8, "v_w01", 7.5)))
         nc.vector.tensor_copy(planes2[:, V3_AT:W3_AT].bitcast(I32), v3_sc_rows.bitcast(I32))
         for r in range(1, 4):
             nc.sync.dma_start(planes2[r:P:32, :].bitcast(I32), planes2[8 * r:P:32, :].bitcast(I32))
+        w5_sb = load_passes(w5_words, "w5_sb", "w1_raw")
+        for b, u in pairs:
+            for g in range(2):
+                bowl(1, g, b, u)
+        g2 = [round_w2(x2, 2, 0, 0, "V", 0), round_w2(x2, 2, 0, 1, "S", 1)]
+        g21 = staged([P, PACK, P, PACK], BF16, "w2_grouped21", 2)
+        for u in range(2):
+            round_w2(x2, 2, 1, u, "S", None, g21[:, 2 * u:2 * u + 2, :, :])
+        y0 = load_rows(w4[0:K_PASS, :], "w4_raw0", "tab_w0")
+        y1 = load_rows(w4[K_PASS:2 * K_PASS, :], "w4_raw1", "w2_raw0")
+        for b, u in pairs:
+            bat(0, 1, b, u)
+        for piece in g2[:2]:
+            quantise_w2(piece)
+        v_words[1] = [gather_half(t1, list1, g, held([P, 2 * S], U8, "v_w1%d" % g)) for g in range(2)]
+        quantise(g21[:].rearrange("p t m i -> p (t m i)"), w2q[2, 1][0][:], w2q[2, 1][1][:])
+        for g in range(2):
+            for b, u in pairs:
+                bat(1, g, b, u)
+        v2_words[2] = [gather_half(u2, list2, g, held([P, 2 * S], U8, "v2_w2%d" % g)) for g in range(2)]
+        for g in range(2):
+            for b, u in pairs:
+                bowl(2, g, b, u, False, True)
+        v3_words = gather(held([P, 2 * S], U8, "v3_w")[:], t3[:], list3[:], U16)
 
-        g = [pair("g00", 0), pair("g01", 2)]
-        for b in range(2):
-            for hh in range(2):
-                round_w2(x0, b, hh, "S", g[b][hh])
-        for hh in range(2):
-            quantise_w2(0, 0, hh, g[0][hh])
-        v2_words[0] = gather_whole(u0, list2, "v2_w0", 0)
-        for hh in range(2):
-            quantise_w2(0, 1, hh, g[1][hh])
-        v_words[0] = [gather_half(t0, list1, 0, "v_w00", 2)]
-        w5_sb = load_passes(w5_words, "w5_sb", "w2_raw0")
-        for b in range(2):
-            for c in range(CHUNKS):
-                bowl_chunk(b, 0, c, True)
-        for b in range(2):
-            for c in range(2):
-                bat_chunk(b, 0, c)
-        g = [pair("g10", 4), pair("g11", 6)]
-        for b in range(2):
-            for hh in range(2):
-                round_w2(x1, b, hh, "S", g[b][hh])
-        for hh in range(2):
-            quantise_w2(1, 0, hh, g[0][hh])
-        v2_words[1] = gather_whole(u1, list2, "v2_w1", 4)
-        for hh in range(2):
-            quantise_w2(1, 1, hh, g[1][hh])
-        y0 = load_rows(w4[0:K_PASS, :], "w4_raw0", "tab2_w1")
-        y1 = load_rows(w4[K_PASS:2 * K_PASS, :], "w4_raw1", "w2_raw1")
-        for b in range(2):
-            for c in range(CHUNKS):
-                bowl_chunk(b, 1, c)
-        g20 = [round_w2(x2, 0, 0, "V", single("g200", 6)), round_w2(x2, 0, 1, "S", single("g201", 8))]
-        g21 = pair("g21", 9)
-        for hh in range(2):
-            round_w2(x2, 1, hh, "S", g21[hh])
-        v_words[0].append(gather_half(t0, list1, 1, "v_w01", 7))
-        for b in range(2):
-            for c in range(2, 4):
-                bat_chunk(b, 0, c)
-        for hh in range(2):
-            quantise_w2(2, 0, hh, g20[hh])
-        v_words[1] = [gather_half(t1, list1, 0, "v_w10", 8), gather_half(t1, list1, 1, "v_w11", 8.5)]
-        for hh in range(2):
-            quantise_w2(2, 1, hh, g21[hh])
-        for c in range(CHUNKS):
-            bat_chunk(0, 1, c)
-        v2_words[2] = [gather_half(u2, list2, 0, "v2_w20", 9), gather_half(u2, list2, 1, "v2_w21", 10)]
-        for c in range(CHUNKS):
-            bowl_chunk(0, 2, c, False, True)
-        for c in range(CHUNKS):
-            bat_chunk(1, 1, c)
-            bowl_chunk(1, 2, c, False, True)
-        v3_words = gather(held([P, 2 * S], U8, "v3_w", "tab2_w2")[:], t3[:], list3[:], U16)
-        d = [[evacuate(b, half, 11 + 2 * b + half) for half in range(2)] for b in range(2)]
+        quarters = [(g, b) for g in range(2) for b in range(2)]
+        d = {(g, b): evacuate(g, b, 8 + 2 * g + b) for g, b in quarters}
+
         def bank(k):
             return psum.tile([P, S], F32, name="bank%d" % k)
 
-        out_banks = [[(0, 256, bank(0)), (256, S, bank(4))], [(0, S, bank(1))], [(0, S, bank(2))], [(0, 256, bank(3)), (256, S, bank(5))]]
+        out_banks = [[(0, HALF, bank(0)), (HALF, S, bank(4))], [(0, S, bank(1))], [(0, S, bank(2))], [(0, HALF, bank(3)), (HALF, S, bank(5))]]
         for n in range(N_TILES):
-            ground_pass(n, 0, S if n in (1, 2) else 256)
-        surplus(0, 0, d[0][0], 23, slice(0, 1))
-        surplus(0, 0, d[0][0], 15, slice(1, 2))
-        surplus(0, 1, d[0][1], 17)
-        for n in (0, 3):
-            ground_pass(n, 256, S)
-        for n in range(N_TILES):
-            hn_pass(0, n, 0, S)
-        surplus(1, 0, d[1][0], 19)
-        a01 = round_w4(0, range(0, 2), y0, "S", 10)
-        b1 = round_w4(1, range(1, 2), y1, "S", 25)
-        b2 = round_w4(1, range(2, 3), y1, "S", 25.5)
-        b3 = round_w4(1, range(3, 4), y1, "S", 14)
-        for n in range(N_TILES):
-            hn_pass(1, n, 0, 256)
-        surplus(1, 1, d[1][1], 21)
-        b0 = round_w4(1, range(0, 1), y1, "V", 22)
-        for n in range(N_TILES):
-            hn_pass(1, n, 256, S)
-        quantise_w4(a01, 21)
-        quantise_w4(b0)
-        quantise_w4(b1, 10)
+            ground_pass(n, 0, S if len(out_banks[n]) == 1 else HALF)
+        for k, (g, b) in enumerate(quarters):
+            surplus(g, b, d[g, b], 12 + 2 * k)
+            if (g, b) == (1, 0):
+                for n in (0, 3):
+                    ground_pass(n, HALF, S)
+            for n in range(N_TILES):
+                hn_pass(b, n, g)
+        a01 = round_w4(0, range(0, 2), y0, "S", 0)
+        a2 = round_w4(0, range(2, 3), y0, "S", 1)
+        a3 = round_w4(0, range(3, 4), y0, "S", 1.5)
+        quantise_w4(a01)
         for n in range(2):
-            hp_pass(0, n, 0, S)
-            hp_pass(1, n, 0, S, True)
-        a2 = round_w4(0, range(2, 3), y0, "V", 22)
-        quantise_w4(b2, 25)
-        quantise_w4(a2)
-        a3 = round_w4(0, range(3, 4), y0, "V", 25.5)
-        quantise_w4(b3, 22)
-        quantise_w4(a3)
+            hp_pass(0, n)
+        b0 = round_w4(1, range(0, 1), y1, "V", 2)
+        b1 = round_w4(1, range(1, 2), y1, "V", 2.5)
+        quantise_w4(b0)
+        quantise_w4(b1)
+        for n in range(2):
+            hp_pass(1, n, True)
+        b2 = round_w4(1, range(2, 3), y1, "V", 3)
+        quantise_w4(a2, 2)
+        quantise_w4(b2)
+        b3 = round_w4(1, range(3, 4), y1, "V", 3.5)
+        quantise_w4(a3, 2.5)
+        quantise_w4(b3)
         for n in range(2, 4):
-            hp_pass(1, n, 0, S)
-            hp_pass(0, n, 0, S, True)
+            hp_pass(0, n)
+            hp_pass(1, n, True)
         for n, piece, engine in ((0, 0, "S"), (0, 1, "S"), (1, 0, "S"), (2, 0, "S"), (3, 0, "V"), (3, 1, "S")):
             finish(n, piece, engine)

@@ -111,11 +111,11 @@ def tile_list_fixture_surplus_scores_kernel(
         w2q = {(a, b): (held([P, K_PASS], U32, "w2_codes%d%d" % (a, b)), held([P, K_PASS], U8, "w2_scales%d%d" % (a, b)))
                for a in range(3) for b in range(2)}
 
-        def round_w2(raw, a, b, u, engine, slot, dst=None):
+        def round_w2(raw, a, b, u, engine, slot, dst=None, rows=slice(0, P)):
             if dst is None:
                 dst = staged([P, 2, P, PACK], BF16, "w2_grouped%d%d%d" % (a, b, u), slot)[:]
-            src = raw[:, :, b * K_PASS:(b + 1) * K_PASS].rearrange("p i (m t) -> p m i t", t=PACK)[:, :, :, 2 * u:2 * u + 2]
-            cast(engine, dst.rearrange("p t m i -> p m i t"), src, -1.0)
+            src = raw[:, :, b * K_PASS:(b + 1) * K_PASS].rearrange("p i (m t) -> p m i t", t=PACK)[:, rows, :, 2 * u:2 * u + 2]
+            cast(engine, dst.rearrange("p t m i -> p m i t")[:, rows, :, :], src, -1.0)
             return a, b, u, dst
 
         def quantise_w2(piece):
@@ -228,10 +228,10 @@ def tile_list_fixture_surplus_scores_kernel(
         x0 = load_w2(0)
         list2 = load_list(offs2, "list2")
         list3 = load_list(offs3, "list3")
-        load_spread(tab3_sc[0:P:8, :], tab3_scales)
+        load_spread(tab3_sc[4:P:8, :], tab3_scales)
         u0 = load_bytes(tab_pass(tab2_words, 0), "tab2_w0")
-        load_spread(planes2[0:P:8, W5_AT:V3_AT].rearrange("p (a c) -> p a c", a=2), w5_scales)
-        load_spread(planes2[0:P:8, W3_AT:SECOND_END], w3_scales)
+        load_spread(planes2[4:P:8, W5_AT:V3_AT].rearrange("p (a c) -> p a c", a=2), w5_scales)
+        load_spread(planes2[4:P:8, W3_AT:SECOND_END], w3_scales)
         t0 = load_bytes(tab_pass(tab_words, 0), "tab_w0")
 
         v_sc_rows = gather(held([P, S], U8, "v_sc_rows")[:], tab_sc[:], list1[:], U8)
@@ -275,16 +275,17 @@ def tile_list_fixture_surplus_scores_kernel(
         v3_sc_rows = gather(staged([P, S], U8, "v3_sc_rows", 7)[:], tab3_sc[:], list3[:], U8)
         v_words[0].append(gather_half(t0, list1, 1, staged([P, 2 * S], U8, "v_w01", 7.5)))
         nc.vector.tensor_copy(planes2[:, V3_AT:W3_AT].bitcast(I32), v3_sc_rows.bitcast(I32))
-        for r in range(1, 4):
-            nc.sync.dma_start(planes2[r:P:32, :].bitcast(I32), planes2[8 * r:P:32, :].bitcast(I32))
+        for r in range(4):
+            nc.sync.dma_start(planes2[r:P:32, :].bitcast(I32), planes2[8 * r + 4:P:32, :].bitcast(I32))
         w5_sb = load_passes(w5_words, "w5_sb", "w1_raw")
         for b, u in pairs:
             for g in range(2):
                 bowl(1, g, b, u)
         g2 = [round_w2(x2, 2, 0, 0, "V", 0), round_w2(x2, 2, 0, 1, "S", 1)]
         g21 = staged([P, PACK, P, PACK], BF16, "w2_grouped21", 2)
-        for u in range(2):
-            round_w2(x2, 2, 1, u, "S", None, g21[:, 2 * u:2 * u + 2, :, :])
+        round_w2(x2, 2, 1, 0, "S", None, g21[:, 0:2, :, :])
+        round_w2(x2, 2, 1, 1, "S", None, g21[:, 2:4, :, :], slice(0, P // 2))
+        round_w2(x2, 2, 1, 1, "V", None, g21[:, 2:4, :, :], slice(P // 2, P))
         y0 = load_rows(w4[0:K_PASS, :], "w4_raw0", "tab_w0")
         y1 = load_rows(w4[K_PASS:2 * K_PASS, :], "w4_raw1", "w2_raw0")
         for b, u in pairs:
@@ -339,5 +340,9 @@ def tile_list_fixture_surplus_scores_kernel(
         for n in range(2, 4):
             hp_pass(0, n)
             hp_pass(1, n, True)
-        for n, piece, engine in ((0, 0, "S"), (0, 1, "S"), (1, 0, "S"), (2, 0, "S"), (3, 0, "V"), (3, 1, "S")):
-            finish(n, piece, engine)
+        for n, piece in ((0, 0), (0, 1), (1, 0), (2, 0)):
+            finish(n, piece, "S")
+        last = held([P, S], F32, "result3")
+        nc.vector.tensor_copy(last[:, 0:HALF], out_banks[3][0][2][:, 0:HALF])
+        nc.scalar.copy(last[:, HALF:S], out_banks[3][1][2][:, 0:HALF])
+        nc.sync.dma_start(out[3 * P:4 * P, :], last[:])

@@ -55,8 +55,8 @@ def tile_list_fixture_surplus_scores_kernel(
         planes2 = held([P, SECOND_END], U8, "planes2")
         nc.vector.memset(planes2[:, W5_AT:V3_AT].bitcast(I32), 0)
         nc.vector.memset(planes2[:, W3_AT:SECOND_END].bitcast(I32), 0)
-        planes1 = zeroed([P, 2 * FIRST_END], "planes1", nc.vector)
         rows1 = held([P, FIRST_END], U8, "rows1")
+        planes1 = [rows1, zeroed([P, FIRST_END], "planes1", nc.vector)]
 
         def load_list(src, name):
             tile = keep.tile([P, S // 16], U16, name=name)
@@ -140,9 +140,8 @@ def tile_list_fixture_surplus_scores_kernel(
         def bat(a, g, b, u):
             for e in range(2):
                 col = b * K_PASS + (2 * u + e) * P
-                at = a * FIRST_END
-                mx(d_banks[g, b, u][:, e, :], w1_perm[:, a, 2 * col:2 * (col + P)], planes1[:, at + W1_AT + col:at + W1_AT + col + P], E2M1,
-                   v_words[a][g], planes1[:, at + V_AT + g * HALF:at + V_AT + (g + 1) * HALF], E4M3, False, False)
+                mx(d_banks[g, b, u][:, e, :], w1_perm[:, a, 2 * col:2 * (col + P)], planes1[a][:, W1_AT + col:W1_AT + col + P], E2M1,
+                   v_words[a][g], planes1[a][:, V_AT + g * HALF:V_AT + (g + 1) * HALF], E4M3, False, False)
 
         h = {(b, s): (held([P, S], U32, "h_codes%d%d" % (b, s)), held([P, S], U8, "h_scales%d%d" % (b, s)))
              for b in range(2) for s in range(2)}
@@ -238,9 +237,9 @@ def tile_list_fixture_surplus_scores_kernel(
         nc.vector.tensor_copy(rows1[:, W1_AT:V_AT].rearrange("p (b t m) -> p b t m", t=PACK, m=P),
                               w1_sc_raw[:].rearrange("p (b m t) -> p b t m", t=PACK, m=P))
         nc.vector.tensor_copy(rows1[:, V_AT:FIRST_END].bitcast(I32), v_sc_rows.bitcast(I32))
-        for q in range(4):
-            nc.gpsimd.dma_start(planes1[32 * q:32 * q + 4, :].rearrange("p (a c) -> p a c", a=2).bitcast(I32),
-                                rows1[32 * q:32 * q + 32:4, :].bitcast(I32))
+        for a in range(2):
+            for r in range(1 - a, 4):
+                nc.gpsimd.dma_start(planes1[a][r:P:32, :].bitcast(I32), rows1[8 * r + 4 * a:P:32, :].bitcast(I32))
         w1_perm = held([P, 2, 2048], U8, "w1_perm")
         for a in range(2):
             nc.vector.tensor_copy(w1_perm[:, a, :].bitcast(U16).rearrange("p (b t m) -> p b t m", t=PACK, m=P),

@@ -137,11 +137,11 @@ def tile_list_fixture_surplus_scores_kernel(
                 mx(d_banks[g, b, u][:, e, :], codes[:, cols], scales[:, cols], E4M3,
                    v2_words[a][g], v2_sc[4 * (a + 1):P, g * HALF:(g + 1) * HALF], E4M3, first and e == 0, last and e == 1)
 
-        def bat(a, g, b, u):
+        def bat(a, g, b, u, last=False):
             for e in range(2):
                 col = b * K_PASS + (2 * u + e) * P
                 mx(d_banks[g, b, u][:, e, :], w1_perm[:, a, 2 * col:2 * (col + P)], planes1[a][:, W1_AT + col:W1_AT + col + P], E2M1,
-                   v_words[a][g], planes1[a][:, V_AT + g * HALF:V_AT + (g + 1) * HALF], E4M3, False, False)
+                   v_words[a][g], planes1[a][:, V_AT + g * HALF:V_AT + (g + 1) * HALF], E4M3, False, last and e == 1)
 
         h = {(b, s): (held([P, S], U32, "h_codes%d%d" % (b, s)), held([P, S], U8, "h_scales%d%d" % (b, s)))
              for b in range(2) for s in range(2)}
@@ -237,9 +237,8 @@ def tile_list_fixture_surplus_scores_kernel(
         nc.vector.tensor_copy(rows1[:, W1_AT:V_AT].rearrange("p (b t m) -> p b t m", t=PACK, m=P),
                               w1_sc_raw[:].rearrange("p (b m t) -> p b t m", t=PACK, m=P))
         nc.vector.tensor_copy(rows1[:, V_AT:FIRST_END].bitcast(I32), v_sc_rows.bitcast(I32))
-        for a in range(2):
-            for r in range(1 - a, 4):
-                nc.gpsimd.dma_start(planes1[a][r:P:32, :].bitcast(I32), rows1[8 * r + 4 * a:P:32, :].bitcast(I32))
+        for r in range(1, 4):
+            nc.gpsimd.dma_start(rows1[r:P:32, :].bitcast(I32), rows1[8 * r:P:32, :].bitcast(I32))
         w1_perm = held([P, 2, 2048], U8, "w1_perm")
         for a in range(2):
             nc.vector.tensor_copy(w1_perm[:, a, :].bitcast(U16).rearrange("p (b t m) -> p b t m", t=PACK, m=P),
@@ -255,7 +254,7 @@ def tile_list_fixture_surplus_scores_kernel(
         for piece in g0[2:]:
             quantise_w2(piece)
         v2_sc = gather(staged([P, S], U8, "v2_sc", 20)[:], tab2_sc[:], list2[:], U8)
-        t1 = load_bytes(tab_pass(tab_words, 1), "tab_w1", "tab2_sc")
+        u2 = load_bytes(tab_pass(tab2_words, 2), "tab2_w2", "tab2_sc")
         v_words[0] = [gather_half(t0, list1, 0, held([P, 2 * S], U8, "v_w00"))]
         for b, u in pairs:
             for g in range(2):
@@ -265,7 +264,9 @@ def tile_list_fixture_surplus_scores_kernel(
         g1 = [round_w2(x1, 1, b, u, "S", 21 if (b, u) == (0, 0) else 4 + 2 * b + u) for b, u in pairs]
         for piece in g1[:2]:
             quantise_w2(piece)
-        u2 = load_bytes(tab_pass(tab2_words, 2), "tab2_w2", slot=21)
+        t1 = load_bytes(tab_pass(tab_words, 1), "tab_w1", slot=21)
+        for r in range(4):
+            nc.sync.dma_start(planes1[1][r:P:32, :].bitcast(I32), rows1[8 * r + 4:P:32, :].bitcast(I32))
         t3 = load_bytes(tab3_words[0], "tab3_w", slot=5)
         v2_words[1] = gather_whole(u1, list2, held([P, 4 * S], U8, "v2_w1"))
         w3_sb = load_bytes(tab_pass(w3_words, 0), "w3_sb", "tab2_w1")
@@ -274,9 +275,9 @@ def tile_list_fixture_surplus_scores_kernel(
         v3_sc_rows = gather(staged([P, S], U8, "v3_sc_rows", 7)[:], tab3_sc[:], list3[:], U8)
         v_words[0].append(gather_half(t0, list1, 1, staged([P, 2 * S], U8, "v_w01", 7.5)))
         nc.vector.tensor_copy(planes2[:, V3_AT:W3_AT].bitcast(I32), v3_sc_rows.bitcast(I32))
+        w5_sb = load_passes(w5_words, "w5_sb", "w1_raw")
         for r in range(4):
             nc.sync.dma_start(planes2[r:P:32, :].bitcast(I32), planes2[8 * r + 4:P:32, :].bitcast(I32))
-        w5_sb = load_passes(w5_words, "w5_sb", "w1_raw")
         for b, u in pairs:
             for g in range(2):
                 bowl(1, g, b, u)
@@ -291,15 +292,16 @@ def tile_list_fixture_surplus_scores_kernel(
             bat(0, 1, b, u)
         for piece in g2[:2]:
             quantise_w2(piece)
-        v_words[1] = [gather_half(t1, list1, g, held([P, 2 * S], U8, "v_w1%d" % g)) for g in range(2)]
-        quantise(g21[:].rearrange("p t m i -> p (t m i)"), w2q[2, 1][0][:], w2q[2, 1][1][:])
-        for g in range(2):
-            for b, u in pairs:
-                bat(1, g, b, u)
         v2_words[2] = [gather_half(u2, list2, g, held([P, 2 * S], U8, "v2_w2%d" % g)) for g in range(2)]
+        quantise(g21[:].rearrange("p t m i -> p (t m i)"), w2q[2, 1][0][:], w2q[2, 1][1][:])
+        for b in range(2):
+            for g in range(2):
+                for u in range(2):
+                    bowl(2, g, b, u)
+        v_words[1] = [gather_half(t1, list1, g, held([P, 2 * S], U8, "v_w1%d" % g)) for g in range(2)]
         for g in range(2):
             for b, u in pairs:
-                bowl(2, g, b, u, False, True)
+                bat(1, g, b, u, True)
         v3_words = gather(held([P, 2 * S], U8, "v3_w")[:], t3[:], list3[:], U16)
 
         quarters = [(g, b) for g in range(2) for b in range(2)]

@@ -23,7 +23,7 @@ FLOPS = 2 * S * (1024 * 1024 + 1536 * 1024 + 2 * 1024 * 512 + 512 * 512)
 
 SLOT = 2048
 
-W1_AT, V_AT, FIRST_END = 0, 1024, 1536
+W1_AT, V_AT, V2_AT, V2_LAST_AT, FIRST_END = 0, 1024, 1536, 2048, 2560
 W5_AT, V3_AT, W3_AT, SECOND_END = 0, 1024, 1536, 2048
 
 
@@ -50,13 +50,13 @@ def tile_list_fixture_surplus_scores_kernel(
 
         tab_sc = zeroed([P, 2048], "tab_sc", nc.vector)
         w1_sc_raw = zeroed([P, 1024], "w1_sc_raw", nc.vector)
-        tab2_sc = zeroed([P, 2048], "tab2_sc", nc.gpsimd)
+        tab2_sc = [zeroed([P, 2048], "tab2_sc%d" % k, nc.vector) for k in range(2)]
         tab3_sc = zeroed([P, 1024], "tab3_sc", nc.vector)
         planes2 = held([P, SECOND_END], U8, "planes2")
         nc.vector.memset(planes2[:, W5_AT:V3_AT].bitcast(I32), 0)
         nc.vector.memset(planes2[:, W3_AT:SECOND_END].bitcast(I32), 0)
         rows1 = held([P, FIRST_END], U8, "rows1")
-        planes1 = [rows1, zeroed([P, FIRST_END], "planes1", nc.vector)]
+        planes1 = [rows1, zeroed([P, V2_AT], "planes1", nc.vector)]
 
         def load_list(src, name):
             tile = keep.tile([P, S // 16], U16, name=name)
@@ -132,10 +132,11 @@ def tile_list_fixture_surplus_scores_kernel(
 
         def bowl(a, g, b, u, first=False, last=False):
             codes, scales = w2q[a, b]
+            first_row, at = ((0, V2_AT), (4, V2_AT), (4, V2_LAST_AT))[a]
             for e in range(2):
                 cols = slice((2 * u + e) * P, (2 * u + e + 1) * P)
                 mx(d_banks[g, b, u][:, e, :], codes[:, cols], scales[:, cols], E4M3,
-                   v2_words[a][g], v2_sc[4 * (a + 1):P, g * HALF:(g + 1) * HALF], E4M3, first and e == 0, last and e == 1)
+                   v2_words[a][g], rows1[first_row:P, at + g * HALF:at + (g + 1) * HALF], E4M3, first and e == 0, last and e == 1)
 
         def bat(a, g, b, u, last=False):
             for e in range(2):
@@ -218,14 +219,14 @@ def tile_list_fixture_surplus_scores_kernel(
         v_words, v2_words = {}, {}
         pairs = [(b, u) for b in range(2) for u in range(2)]
 
-        for q in range(4):
-            nc.gpsimd.dma_start(tab2_sc[32 * q + 4:32 * q + 16, :].bitcast(I32), tab2_scales[:, 4 * q:4 * q + 4, :].bitcast(I32))
         w1_raw = load_passes(w1_words, "w1_raw")
         list1 = load_list(offs, "list1")
         load_spread(tab_sc[0:P:4, :], tab_scales)
         load_spread(w1_sc_raw[0:P:4, :], w1_scales)
-        x0 = load_w2(0)
         list2 = load_list(offs2, "list2")
+        load_spread(tab2_sc[0][0:P:4, :], tab2_scales[0:2])
+        x0 = load_w2(0)
+        load_spread(tab2_sc[1][4:P:8, :], tab2_scales[2:3])
         list3 = load_list(offs3, "list3")
         load_spread(tab3_sc[4:P:8, :], tab3_scales)
         u0 = load_bytes(tab_pass(tab2_words, 0), "tab2_w0")
@@ -236,9 +237,12 @@ def tile_list_fixture_surplus_scores_kernel(
         v_sc_rows = gather(held([P, S], U8, "v_sc_rows")[:], tab_sc[:], list1[:], U8)
         nc.vector.tensor_copy(rows1[:, W1_AT:V_AT].rearrange("p (b t m) -> p b t m", t=PACK, m=P),
                               w1_sc_raw[:].rearrange("p (b m t) -> p b t m", t=PACK, m=P))
-        nc.vector.tensor_copy(rows1[:, V_AT:FIRST_END].bitcast(I32), v_sc_rows.bitcast(I32))
-        for r in range(1, 4):
-            nc.gpsimd.dma_start(rows1[r:P:32, :].bitcast(I32), rows1[8 * r:P:32, :].bitcast(I32))
+        nc.vector.tensor_copy(rows1[:, V_AT:V2_AT].bitcast(I32), v_sc_rows.bitcast(I32))
+        for k, (first, cols) in enumerate(((0, slice(W1_AT, V2_LAST_AT)), (4, slice(V2_AT, FIRST_END)))):
+            v2_sc_rows = gather(held([P, S], U8, "v2_sc_rows%d" % k)[:], tab2_sc[k][:], list2[:], U8)
+            nc.vector.tensor_copy(rows1[:, V2_AT + k * S:V2_AT + (k + 1) * S].bitcast(I32), v2_sc_rows.bitcast(I32))
+            for r in range(1, 4):
+                nc.gpsimd.dma_start(rows1[first + r:P:32, cols].bitcast(I32), rows1[first + 8 * r:P:32, cols].bitcast(I32))
         w1_perm = held([P, 2, 2048], U8, "w1_perm")
         for a in range(2):
             nc.vector.tensor_copy(w1_perm[:, a, :].bitcast(U16).rearrange("p (b t m) -> p b t m", t=PACK, m=P),
@@ -246,15 +250,14 @@ def tile_list_fixture_surplus_scores_kernel(
         x1 = load_w2(1, "w1_raw")
         u1 = load_bytes(tab_pass(tab2_words, 1), "tab2_w1")
 
-        g0 = [round_w2(x0, 0, b, u, "S", 20 if (b, u) == (1, 1) else 2 * b + u) for b, u in pairs]
+        g0 = [round_w2(x0, 0, b, u, "S", 2 * b + u) for b, u in pairs]
         x2 = load_w2(2, "w2_raw0")
         for piece in g0[:2]:
             quantise_w2(piece)
         v2_words[0] = gather_whole(u0, list2, held([P, 4 * S], U8, "v2_w0"))
         for piece in g0[2:]:
             quantise_w2(piece)
-        v2_sc = gather(staged([P, S], U8, "v2_sc", 20)[:], tab2_sc[:], list2[:], U8)
-        u2 = load_bytes(tab_pass(tab2_words, 2), "tab2_w2", "tab2_sc")
+        u2 = load_bytes(tab_pass(tab2_words, 2), "tab2_w2", "tab2_sc1")
         v_words[0] = [gather_half(t0, list1, 0, held([P, 2 * S], U8, "v_w00"))]
         for b, u in pairs:
             for g in range(2):
@@ -266,7 +269,7 @@ def tile_list_fixture_surplus_scores_kernel(
             quantise_w2(piece)
         t1 = load_bytes(tab_pass(tab_words, 1), "tab_w1", slot=21)
         for r in range(4):
-            nc.sync.dma_start(planes1[1][r:P:32, :].bitcast(I32), rows1[8 * r + 4:P:32, :].bitcast(I32))
+            nc.sync.dma_start(planes1[1][r:P:32, :].bitcast(I32), rows1[8 * r + 4:P:32, W1_AT:V2_AT].bitcast(I32))
         t3 = load_bytes(tab3_words[0], "tab3_w", slot=5)
         v2_words[1] = gather_whole(u1, list2, held([P, 4 * S], U8, "v2_w1"))
         w3_sb = load_bytes(tab_pass(w3_words, 0), "w3_sb", "tab2_w1")

@@ -127,7 +127,7 @@ def tile_list_fixture_surplus_scores_kernel(
             nc.tensor.matmul_mx(out=dst, lhsT=lhsT.bitcast(lhsT_fmt), lhsT_scale=lhsT_scale,
                                 rhs=rhs.bitcast(rhs_fmt), rhs_scale=rhs_scale, start=start, stop=stop)
 
-        d_banks = {(g, b, u): psum.tile([P, 2, HALF], F32, name="bank%d" % (4 * g + 2 * b + u))
+        d_banks = {(g, b, u): psum.tile([P, 2, HALF], F32, name="bank%d" % (4 * b + 2 * g + u))
                    for g in range(2) for b in range(2) for u in range(2)}
 
         def bowl(a, g, b, u, first=False, last=False):
@@ -227,11 +227,11 @@ def tile_list_fixture_surplus_scores_kernel(
         load_spread(tab2_sc[0][0:P:4, :], tab2_scales[0:2])
         x0 = load_w2(0)
         load_spread(tab2_sc[1][4:P:8, :], tab2_scales[2:3])
+        load_spread(tab3_sc[0:P:8, :], tab3_scales)
+        load_spread(planes2[0:P:8, W5_AT:V3_AT].rearrange("p (a c) -> p a c", a=2), w5_scales)
+        load_spread(planes2[0:P:8, W3_AT:SECOND_END], w3_scales)
         list3 = load_list(offs3, "list3")
-        load_spread(tab3_sc[4:P:8, :], tab3_scales)
         u0 = load_bytes(tab_pass(tab2_words, 0), "tab2_w0")
-        load_spread(planes2[4:P:8, W5_AT:V3_AT].rearrange("p (a c) -> p a c", a=2), w5_scales)
-        load_spread(planes2[4:P:8, W3_AT:SECOND_END], w3_scales)
         t0 = load_bytes(tab_pass(tab_words, 0), "tab_w0")
 
         v_sc_rows = gather(held([P, S], U8, "v_sc_rows")[:], tab_sc[:], list1[:], U8)
@@ -279,8 +279,8 @@ def tile_list_fixture_surplus_scores_kernel(
         v_words[0].append(gather_half(t0, list1, 1, staged([P, 2 * S], U8, "v_w01", 7.5)))
         nc.vector.tensor_copy(planes2[:, V3_AT:W3_AT].bitcast(I32), v3_sc_rows.bitcast(I32))
         w5_sb = load_passes(w5_words, "w5_sb", "w1_raw")
-        for r in range(4):
-            nc.sync.dma_start(planes2[r:P:32, :].bitcast(I32), planes2[8 * r + 4:P:32, :].bitcast(I32))
+        for r in range(1, 4):
+            nc.sync.dma_start(planes2[r:P:32, :].bitcast(I32), planes2[8 * r:P:32, :].bitcast(I32))
         for b, u in pairs:
             for g in range(2):
                 bowl(1, g, b, u)
@@ -297,17 +297,20 @@ def tile_list_fixture_surplus_scores_kernel(
             quantise_w2(piece)
         v2_words[2] = [gather_half(u2, list2, g, held([P, 2 * S], U8, "v2_w2%d" % g)) for g in range(2)]
         quantise(g21[:].rearrange("p t m i -> p (t m i)"), w2q[2, 1][0][:], w2q[2, 1][1][:])
-        for b in range(2):
-            for g in range(2):
-                for u in range(2):
-                    bowl(2, g, b, u)
         v_words[1] = [gather_half(t1, list1, g, held([P, 2 * S], U8, "v_w1%d" % g)) for g in range(2)]
         for g in range(2):
-            for b, u in pairs:
-                bat(1, g, b, u, True)
+            for u in range(2):
+                bowl(2, g, 0, u)
+        for g in range(2):
+            for u in range(2):
+                bat(1, g, 0, u, True)
+        for g in range(2):
+            for u in range(2):
+                bat(1, g, 1, u)
+                bowl(2, g, 1, u, False, True)
         v3_words = gather(held([P, 2 * S], U8, "v3_w")[:], t3[:], list3[:], U16)
 
-        quarters = [(g, b) for g in range(2) for b in range(2)]
+        quarters = [(g, b) for b in range(2) for g in range(2)]
         d = {(g, b): evacuate(g, b, 8 + 2 * g + b) for g, b in quarters}
 
         def bank(k):
@@ -318,7 +321,7 @@ def tile_list_fixture_surplus_scores_kernel(
             ground_pass(n, 0, S if len(out_banks[n]) == 1 else HALF)
         for k, (g, b) in enumerate(quarters):
             surplus(g, b, d[g, b], 12 + 2 * k)
-            if (g, b) == (1, 0):
+            if k == 1:
                 for n in (0, 3):
                     ground_pass(n, HALF, S)
             for n in range(N_TILES):

@@ -242,7 +242,7 @@ def tile_list_fixture_surplus_scores_kernel(
             v2_sc_rows = gather(held([P, S], U8, "v2_sc_rows%d" % k)[:], tab2_sc[k][:], list2[:], U8)
             nc.vector.tensor_copy(rows1[:, V2_AT + k * S:V2_AT + (k + 1) * S].bitcast(I32), v2_sc_rows.bitcast(I32))
             for r in range(1, 4):
-                nc.gpsimd.dma_start(rows1[first + r:P:32, cols].bitcast(I32), rows1[first + 8 * r:P:32, cols].bitcast(I32))
+                nc.sync.dma_start(rows1[first + r:P:32, cols].bitcast(I32), rows1[first + 8 * r:P:32, cols].bitcast(I32))
         w1_perm = held([P, 2, 2048], U8, "w1_perm")
         for a in range(2):
             nc.vector.tensor_copy(w1_perm[:, a, :].bitcast(U16).rearrange("p (b t m) -> p b t m", t=PACK, m=P),

@@ -341,7 +341,7 @@ def tile_list_fixture_surplus_scores_kernel(
         b2 = round_w4(1, range(2, 3), y1, "V", 3)
         quantise_w4(a2, 2)
         quantise_w4(b2)
-        b3 = round_w4(1, range(3, 4), y1, "V", 3.5)
+        b3 = round_w4(1, range(3, 4), y1, "S", 3.5)
         quantise_w4(a3, 2.5)
         quantise_w4(b3)
         for n in range(2, 4):

from contextlib import ExitStack

import concourse.mybir as mybir

F32 = mybir.dt.float32
BF16 = mybir.dt.bfloat16
I32 = mybir.dt.int32
U32 = mybir.dt.uint32
U16 = mybir.dt.uint16
U8 = mybir.dt.uint8
E4M3 = mybir.dt.float8_e4m3fn_x4
E2M1 = mybir.dt.float4_e2m1fn_x4
ALU = mybir.AluOpType
ACT = mybir.ActivationFunctionType

P = 128
PACK = 4
K_PASS = P * PACK
S = 512
HALF = S // 2
N_TILES = 4
FLOPS = 2 * S * (1024 * 1024 + 1536 * 1024 + 2 * 1024 * 512 + 512 * 512)

SLOT = 2048

W1_AT, V_AT, V2_AT, V2_LAST_AT, FIRST_END = 0, 1024, 1536, 2048, 2560
W5_AT, V3_AT, W3_AT, SECOND_END = 0, 1024, 1536, 2048


def tile_list_fixture_surplus_scores_kernel(
    tc, tab_words, tab_scales, tab2_words, tab2_scales, tab3_words, tab3_scales, offs, offs2, offs3,
    w1_words, w1_scales, w2, w3_words, w3_scales, w4, w5_words, w5_scales, out,
):
    nc = tc.nc
    with ExitStack() as ctx:
        keep = ctx.enter_context(tc.tile_pool(name="keep", bufs=1))
        stage = ctx.enter_context(tc.tile_pool(name="stage", bufs=1))
        psum = ctx.enter_context(tc.psum_pool(name="psum", bufs=1))

        def held(shape, dtype, name, tag=None):
            return keep.tile(shape, dtype, name=name, tag=tag or name, align_bytes=64)

        def zeroed(shape, name, engine):
            tile = held(shape, U8, name)
            engine.memset(tile[:].bitcast(I32), 0)
            return tile

        def staged(shape, dtype, name, slot):
            return stage.tile(shape, dtype, name=name, offset=int(slot * SLOT), align_bytes=64)

        tab_sc = zeroed([P, 2048], "tab_sc", nc.vector)
        w1_sc_raw = zeroed([P, 1024], "w1_sc_raw", nc.vector)
        tab2_sc = [zeroed([P, 2048], "tab2_sc%d" % k, nc.vector) for k in range(2)]
        tab3_sc = zeroed([P, 1024], "tab3_sc", nc.vector)
        planes2 = held([P, SECOND_END], U8, "planes2")
        nc.vector.memset(planes2[:, W5_AT:V3_AT].bitcast(I32), 0)
        nc.vector.memset(planes2[:, W3_AT:SECOND_END].bitcast(I32), 0)
        rows1 = held([P, FIRST_END], U8, "rows1")
        planes1 = [rows1, zeroed([P, V2_AT], "planes1", nc.vector)]

        def load_list(src, name):
            tile = keep.tile([P, S // 16], U16, name=name)
            nc.sync.dma_start(tile[:], src)
            return tile

        def load_bytes(src, name, tag=None, slot=None):
            shape = [P, src.shape[1]]
            tile = held(shape, U8, name, tag) if slot is None else staged(shape, U8, name, slot)
            nc.sync.dma_start(tile[:].bitcast(I32), src.bitcast(I32))
            return tile

        def load_passes(src, name, tag=None):
            tile = held([P, src.shape[0], src.shape[2]], U8, name, tag)
            nc.sync.dma_start(tile[:].bitcast(I32), src.rearrange("a p c -> p a c").bitcast(I32))
            return tile

        def load_spread(dst, src):
            nc.sync.dma_start(dst.bitcast(I32), src.rearrange("a q c -> q a c").bitcast(I32))

        def load_rows(src, name, tag=None):
            tile = held([P, PACK, src.shape[1]], F32, name, tag)
            nc.sync.dma_start(tile[:], src.rearrange("(p i) c -> p i c", i=PACK))
            return tile

        def load_w2(a, tag=None):
            return load_rows(w2[a * K_PASS:(a + 1) * K_PASS, :], "w2_raw%d" % a, tag)

        def tab_pass(words, a):
            return words[a].rearrange("p t i -> p (t i)")

        def gather(dst, window, offsets, dtype):
            nc.vector.tensor_copy(dst.bitcast(dtype), window.bitcast(dtype).indirect(offsets))
            return dst

        def gather_whole(window, offsets, tile):
            gather(tile[:], window[:], offsets[:], U32)
            return [tile[:, 0:2 * S], tile[:, 2 * S:4 * S]]

        def gather_half(window, offsets, half, tile):
            return gather(tile[:], window[:], offsets[:, 16 * half:16 * (half + 1)], U32)

        def cast(engine, dst, src, factor):
            if engine == "S":
                nc.scalar.activation(dst, src, ACT.Copy, scale=factor)
            else:
                nc.vector.tensor_scalar(dst, src, factor, None, ALU.mult)

        def quantise(grouped, codes, scales):
            nc.vector.quantize_mx(out=codes.bitcast(E4M3), scales=scales, in_=grouped)

        w2q = {(a, b): (held([P, K_PASS], U32, "w2_codes%d%d" % (a, b)), held([P, K_PASS], U8, "w2_scales%d%d" % (a, b)))
               for a in range(3) for b in range(2)}

        def round_w2(raw, a, b, u, engine, slot, dst=None, rows=slice(0, P)):
            if dst is None:
                dst = staged([P, 2, P, PACK], BF16, "w2_grouped%d%d%d" % (a, b, u), slot)[:]
            src = raw[:, :, b * K_PASS:(b + 1) * K_PASS].rearrange("p i (m t) -> p m i t", t=PACK)[:, rows, :, 2 * u:2 * u + 2]
            cast(engine, dst.rearrange("p t m i -> p m i t")[:, rows, :, :], src, -1.0)
            return a, b, u, dst

        def quantise_w2(piece):
            a, b, u, grouped = piece
            cols = slice(2 * u * P, 2 * (u + 1) * P)
            quantise(grouped.rearrange("p t m i -> p (t m i)"), w2q[a, b][0][:, cols], w2q[a, b][1][:, cols])

        def mx(dst, lhsT, lhsT_scale, lhsT_fmt, rhs, rhs_scale, rhs_fmt, start, stop):
            nc.tensor.matmul_mx(out=dst, lhsT=lhsT.bitcast(lhsT_fmt), lhsT_scale=lhsT_scale,
                                rhs=rhs.bitcast(rhs_fmt), rhs_scale=rhs_scale, start=start, stop=stop)

        d_banks = {(g, b, u): psum.tile([P, 2, HALF], F32, name="bank%d" % (4 * b + 2 * g + u))
                   for g in range(2) for b in range(2) for u in range(2)}

        def bowl(a, g, b, u, first=False, last=False):
            codes, scales = w2q[a, b]
            first_row, at = ((0, V2_AT), (4, V2_AT), (4, V2_LAST_AT))[a]
            for e in range(2):
                cols = slice((2 * u + e) * P, (2 * u + e + 1) * P)
                mx(d_banks[g, b, u][:, e, :], codes[:, cols], scales[:, cols], E4M3,
                   v2_words[a][g], rows1[first_row:P, at + g * HALF:at + (g + 1) * HALF], E4M3, first and e == 0, last and e == 1)

        def bat(a, g, b, u, last=False):
            for e in range(2):
                col = b * K_PASS + (2 * u + e) * P
                mx(d_banks[g, b, u][:, e, :], w1_perm[:, a, 2 * col:2 * (col + P)], planes1[a][:, W1_AT + col:W1_AT + col + P], E2M1,
                   v_words[a][g], planes1[a][:, V_AT + g * HALF:V_AT + (g + 1) * HALF], E4M3, False, last and e == 1)

        h = {(b, s): (held([P, S], U32, "h_codes%d%d" % (b, s)), held([P, S], U8, "h_scales%d%d" % (b, s)))
             for b in range(2) for s in range(2)}

        def evacuate(g, b, slot):
            d = staged([P, 2, HALF, 2], BF16, "d%d%d" % (g, b), slot)
            for u in range(2):
                nc.scalar.copy(d[:, u, :, :], d_banks[g, b, u][:].rearrange("p e j -> p j e"))
            return d

        def surplus(g, b, d, slot):
            cols = slice(g * HALF, (g + 1) * HALF)
            parts = []
            for s, op in ((1, ALU.min), (0, ALU.max)):
                part = staged([P, HALF, 2, 2], BF16, "part%d%d%d" % (g, b, s), slot + s)
                nc.vector.tensor_scalar(part[:], d[:].rearrange("p u j e -> p j u e"), 0.0, None, op)
                parts.append((part[:].rearrange("p j u e -> p (j u e)"), h[b, s][0][:, cols], h[b, s][1][:, cols]))
            for part in parts:
                quantise(*part)

        opened = set()

        def out_passes(n, j0, j1, last, run):
            for lo, hi, bank in out_banks[n]:
                a, z = max(lo, j0), min(hi, j1)
                if a < z:
                    run(bank[:, a - lo:z - lo], slice(a, z), (n, lo) not in opened, last)
                    opened.add((n, lo))

        def hp_pass(b, n, last=False):
            codes, scales = w4q[b, n]
            out_passes(n, 0, S, last, lambda dst, cols, start, stop: mx(
                dst, codes, scales, E4M3, h[b, 0][0][:, cols], h[b, 0][1][:, cols], E4M3, start, stop))

        def hn_pass(b, n, g):
            at = W5_AT + b * K_PASS + n * P
            out_passes(n, g * HALF, (g + 1) * HALF, False, lambda dst, cols, start, stop: mx(
                dst, w5_sb[:, b, 2 * n * P:2 * (n + 1) * P], planes2[:, at:at + P], E2M1,
                h[b, 1][0][:, cols], h[b, 1][1][:, cols], E4M3, start, stop))

        def ground_pass(n, j0, j1):
            out_passes(n, j0, j1, False, lambda dst, cols, start, stop: mx(
                dst, w3_sb[:, 4 * n * P:4 * (n + 1) * P], planes2[:, W3_AT + n * P:W3_AT + (n + 1) * P], E4M3,
                v3_words[:, 2 * cols.start:2 * cols.stop], planes2[:, V3_AT + cols.start:V3_AT + cols.stop], E2M1, start, stop))

        def finish(n, piece, engine):
            lo, hi, bank = out_banks[n][piece]
            result = held([P, hi - lo], F32, "result%d%d" % (n, piece))
            if engine == "S":
                nc.scalar.copy(result[:], bank[:, 0:hi - lo])
            else:
                nc.vector.tensor_copy(result[:], bank[:, 0:hi - lo])
            nc.sync.dma_start(out[n * P:(n + 1) * P, lo:hi], result[:])

        w4q = {}

        def round_w4(b, tiles, raw, engine, slot):
            cols = slice(tiles.start * P, tiles.stop * P)
            grouped = staged([P, len(tiles) * P, PACK], BF16, "w4_grouped%d%d" % (b, tiles.start), slot)
            cast(engine, grouped[:].rearrange("p (c e) i -> p c i e", e=4),
                 raw[:, :, cols].rearrange("p i (c e) -> p c i e", e=4), 1.0)
            return b, tiles, grouped

        def quantise_w4(piece, slot=None):
            b, tiles, grouped = piece
            name = "w4_codes%d%d" % (b, tiles.start)
            shape = [P, len(tiles) * P]
            codes = held(shape, U32, name) if slot is None else staged(shape, U32, name, slot)
            scales = held(shape, U8, "w4_scales%d%d" % (b, tiles.start))
            quantise(grouped[:].rearrange("p c i -> p (c i)"), codes[:], scales[:])
            for k, n in enumerate(tiles):
                w4q[b, n] = (codes[:, k * P:(k + 1) * P], scales[:, k * P:(k + 1) * P])

        v_words, v2_words = {}, {}
        pairs = [(b, u) for b in range(2) for u in range(2)]

        w1_raw = load_passes(w1_words, "w1_raw")
        list1 = load_list(offs, "list1")
        load_spread(tab_sc[0:P:4, :], tab_scales)
        load_spread(w1_sc_raw[0:P:4, :], w1_scales)
        list2 = load_list(offs2, "list2")
        load_spread(tab2_sc[0][0:P:4, :], tab2_scales[0:2])
        x0 = load_w2(0)
        load_spread(tab2_sc[1][4:P:8, :], tab2_scales[2:3])
        load_spread(tab3_sc[0:P:8, :], tab3_scales)
        load_spread(planes2[0:P:8, W5_AT:V3_AT].rearrange("p (a c) -> p a c", a=2), w5_scales)
        load_spread(planes2[0:P:8, W3_AT:SECOND_END], w3_scales)
        list3 = load_list(offs3, "list3")
        u0 = load_bytes(tab_pass(tab2_words, 0), "tab2_w0")
        t0 = load_bytes(tab_pass(tab_words, 0), "tab_w0")

        v_sc_rows = gather(held([P, S], U8, "v_sc_rows")[:], tab_sc[:], list1[:], U8)
        nc.vector.tensor_copy(rows1[:, W1_AT:V_AT].rearrange("p (b t m) -> p b t m", t=PACK, m=P),
                              w1_sc_raw[:].rearrange("p (b m t) -> p b t m", t=PACK, m=P))
        nc.vector.tensor_copy(rows1[:, V_AT:V2_AT].bitcast(I32), v_sc_rows.bitcast(I32))
        for k, (first, cols) in enumerate(((0, slice(W1_AT, V2_LAST_AT)), (4, slice(V2_AT, FIRST_END)))):
            v2_sc_rows = gather(held([P, S], U8, "v2_sc_rows%d" % k)[:], tab2_sc[k][:], list2[:], U8)
            nc.vector.tensor_copy(rows1[:, V2_AT + k * S:V2_AT + (k + 1) * S].bitcast(I32), v2_sc_rows.bitcast(I32))
            for r in range(1, 4):
                nc.sync.dma_start(rows1[first + r:P:32, cols].bitcast(I32), rows1[first + 8 * r:P:32, cols].bitcast(I32))
        w1_perm = held([P, 2, 2048], U8, "w1_perm")
        for a in range(2):
            nc.vector.tensor_copy(w1_perm[:, a, :].bitcast(U16).rearrange("p (b t m) -> p b t m", t=PACK, m=P),
                                  w1_raw[:, a, :].bitcast(U16).rearrange("p (b m t) -> p b t m", t=PACK, m=P))
        x1 = load_w2(1, "w1_raw")
        u1 = load_bytes(tab_pass(tab2_words, 1), "tab2_w1")

        g0 = [round_w2(x0, 0, b, u, "S", 2 * b + u) for b, u in pairs]
        x2 = load_w2(2, "w2_raw0")
        for piece in g0[:2]:
            quantise_w2(piece)
        v2_words[0] = gather_whole(u0, list2, held([P, 4 * S], U8, "v2_w0"))
        for piece in g0[2:]:
            quantise_w2(piece)
        u2 = load_bytes(tab_pass(tab2_words, 2), "tab2_w2", "tab2_sc1")
        v_words[0] = [gather_half(t0, list1, 0, held([P, 2 * S], U8, "v_w00"))]
        for b, u in pairs:
            for g in range(2):
                bowl(0, g, b, u, True)
        for b, u in pairs:
            bat(0, 0, b, u)
        g1 = [round_w2(x1, 1, b, u, "S", 21 if (b, u) == (0, 0) else 4 + 2 * b + u) for b, u in pairs]
        for piece in g1[:2]:
            quantise_w2(piece)
        t1 = load_bytes(tab_pass(tab_words, 1), "tab_w1", slot=21)
        for r in range(4):
            nc.sync.dma_start(planes1[1][r:P:32, :].bitcast(I32), rows1[8 * r + 4:P:32, W1_AT:V2_AT].bitcast(I32))
        t3 = load_bytes(tab3_words[0], "tab3_w", slot=5)
        v2_words[1] = gather_whole(u1, list2, held([P, 4 * S], U8, "v2_w1"))
        w3_sb = load_bytes(tab_pass(w3_words, 0), "w3_sb", "tab2_w1")
        for piece in g1[2:]:
            quantise_w2(piece)
        v3_sc_rows = gather(staged([P, S], U8, "v3_sc_rows", 7)[:], tab3_sc[:], list3[:], U8)
        v_words[0].append(gather_half(t0, list1, 1, staged([P, 2 * S], U8, "v_w01", 7.5)))
        nc.vector.tensor_copy(planes2[:, V3_AT:W3_AT].bitcast(I32), v3_sc_rows.bitcast(I32))
        w5_sb = load_passes(w5_words, "w5_sb", "w1_raw")
        for r in range(1, 4):
            nc.sync.dma_start(planes2[r:P:32, :].bitcast(I32), planes2[8 * r:P:32, :].bitcast(I32))
        for b, u in pairs:
            for g in range(2):
                bowl(1, g, b, u)
        g2 = [round_w2(x2, 2, 0, 0, "V", 0), round_w2(x2, 2, 0, 1, "S", 1)]
        g21 = staged([P, PACK, P, PACK], BF16, "w2_grouped21", 2)
        round_w2(x2, 2, 1, 0, "S", None, g21[:, 0:2, :, :])
        round_w2(x2, 2, 1, 1, "S", None, g21[:, 2:4, :, :], slice(0, P // 2))
        round_w2(x2, 2, 1, 1, "V", None, g21[:, 2:4, :, :], slice(P // 2, P))
        y0 = load_rows(w4[0:K_PASS, :], "w4_raw0", "tab_w0")
        y1 = load_rows(w4[K_PASS:2 * K_PASS, :], "w4_raw1", "w2_raw0")
        for b, u in pairs:
            bat(0, 1, b, u)
        for piece in g2[:2]:
            quantise_w2(piece)
        v2_words[2] = [gather_half(u2, list2, g, held([P, 2 * S], U8, "v2_w2%d" % g)) for g in range(2)]
        quantise(g21[:].rearrange("p t m i -> p (t m i)"), w2q[2, 1][0][:], w2q[2, 1][1][:])
        v_words[1] = [gather_half(t1, list1, g, held([P, 2 * S], U8, "v_w1%d" % g)) for g in range(2)]
        for g in range(2):
            for u in range(2):
                bowl(2, g, 0, u)
        for g in range(2):
            for u in range(2):
                bat(1, g, 0, u, True)
        for g in range(2):
            for u in range(2):
                bat(1, g, 1, u)
                bowl(2, g, 1, u, False, True)
        v3_words = gather(held([P, 2 * S], U8, "v3_w")[:], t3[:], list3[:], U16)

        quarters = [(g, b) for b in range(2) for g in range(2)]
        d = {(g, b): evacuate(g, b, 8 + 2 * g + b) for g, b in quarters}

        def bank(k):
            return psum.tile([P, S], F32, name="bank%d" % k)

        out_banks = [[(0, HALF, bank(0)), (HALF, S, bank(4))], [(0, S, bank(1))], [(0, S, bank(2))], [(0, HALF, bank(3)), (HALF, S, bank(5))]]
        for n in range(N_TILES):
            ground_pass(n, 0, S if len(out_banks[n]) == 1 else HALF)
        for k, (g, b) in enumerate(quarters):
            surplus(g, b, d[g, b], 12 + 2 * k)
            if k == 1:
                for n in (0, 3):
                    ground_pass(n, HALF, S)
            for n in range(N_TILES):
                hn_pass(b, n, g)
        a01 = round_w4(0, range(0, 2), y0, "S", 0)
        a2 = round_w4(0, range(2, 3), y0, "S", 1)
        a3 = round_w4(0, range(3, 4), y0, "S", 1.5)
        quantise_w4(a01)
        for n in range(2):
            hp_pass(0, n)
        b0 = round_w4(1, range(0, 1), y1, "V", 2)
        b1 = round_w4(1, range(1, 2), y1, "V", 2.5)
        quantise_w4(b0)
        quantise_w4(b1)
        for n in range(2):
            hp_pass(1, n, True)
        b2 = round_w4(1, range(2, 3), y1, "V", 3)
        quantise_w4(a2, 2)
        quantise_w4(b2)
        b3 = round_w4(1, range(3, 4), y1, "S", 3.5)
        quantise_w4(a3, 2.5)
        quantise_w4(b3)
        for n in range(2, 4):
            hp_pass(0, n)
            hp_pass(1, n, True)
        for n, piece in ((0, 0), (0, 1), (1, 0), (2, 0)):
            finish(n, piece, "S")
        last = held([P, S], F32, "result3")
        nc.vector.tensor_copy(last[:, 0:HALF], out_banks[3][0][2][:, 0:HALF])
        nc.scalar.copy(last[:, HALF:S], out_banks[3][1][2][:, 0:HALF])
        nc.sync.dma_start(out[3 * P:4 * P, :], last[:])
